import numpy as np
import ml_dtypes


def mxq(x, axis, fmt="e4m3"):
    dtype, down = {"e4m3": (ml_dtypes.float8_e4m3fn, 7), "e5m2": (ml_dtypes.float8_e5m2, 14)}[fmt]
    v = np.moveaxis(np.asarray(x, np.float32).astype(ml_dtypes.bfloat16).astype(np.float64), axis, -1)
    blocks = v.reshape(v.shape[:-1] + (-1, 32))
    amax = np.abs(blocks).max(-1, keepdims=True)
    byte = np.maximum(np.where(amax > 0, np.frexp(amax)[1] - 1 + 127, 0) - down, 1)
    scale = np.exp2(byte - 127.0)
    codes = (blocks / scale).astype(np.float32).astype(dtype).astype(np.float64)
    return np.moveaxis((codes * scale).reshape(v.shape), -1, axis)


WIDE = False


def mx_kscale(k):
    if not WIDE:
        return np.ones(k)
    levels = np.array([10, -10, 5, -5, 0])
    if k % 512:
        return np.exp2(np.random.permutation(np.resize(levels, k // 32))).repeat(32)
    a = np.empty((k // 512, 16))
    for p in range(k // 512):
        a[p, :8] = np.random.permutation(np.resize(levels, 8))
        for g in range(8):
            far = levels[np.abs(levels - a[p, g]) >= 10]
            a[p, g + 8] = far[np.random.randint(len(far))]
    return np.exp2(a.ravel()).repeat(32)


def f64(x):
    return np.asarray(x).astype(np.float64)


def striped(idx):
    return np.tile(idx.reshape(-1, 16).T, (8, 1)).astype(np.uint16)


def unstriped(offs):
    return offs[:16].T.reshape(-1).astype(np.int64)


def striped8(idx):
    return np.concatenate([x.reshape(-1, 16).T for x in idx]).astype(np.uint16)


def runs(offs, k):
    lists = np.stack([offs[16 * r : 16 * r + 16].T.reshape(-1) for r in range(8)]).astype(np.int64)
    return lists[np.arange(k) % 512 // 64]


def pack_weight(w):
    k, n = w.shape
    w = f64(np.asarray(w, np.float32).astype(ml_dtypes.bfloat16)).reshape(k // 32, 32, n)
    amax = np.abs(w).max(1)
    byte = np.clip(np.where(amax > 0, np.frexp(amax)[1] - 1 + 127 - 7, 1), 1, 254)
    scaled = (w * np.exp2(127.0 - byte)[:, None, :]).reshape(k, n).astype(np.float32)
    words = np.ascontiguousarray(scaled.reshape(k // 512, 128, 4, n).transpose(0, 1, 3, 2)).astype(ml_dtypes.float8_e4m3fn).view(np.uint8)
    return words, np.ascontiguousarray(byte.astype(np.uint8).reshape(k // 512, 16, n))


def unpack_weight(words, scales):
    g, p, n, _ = words.shape
    vals = np.ascontiguousarray(words).view(ml_dtypes.float8_e4m3fn).astype(np.float64) * np.repeat(np.exp2(scales.astype(np.float64) - 127.0), 8, axis=1)[..., None]
    return vals.transpose(0, 1, 3, 2).reshape(g * 512, n)

def planes(y):
    n, m = y.shape
    v = y.astype(np.float32).astype(ml_dtypes.bfloat16).astype(np.float64).reshape(n // 32, 32, m)
    top = np.abs(v).max(1)
    byte = np.clip(np.where(top > 0, np.frexp(top)[1] - 1 + 127 - 7, 1), 1, 254)
    codes = (v * np.exp2(127.0 - byte)[:, None, :]).reshape(n, m).astype(np.float32).astype(ml_dtypes.float8_e4m3fn).view(np.uint8)
    words = codes.reshape(n // 512, 128, 4, m).transpose(0, 1, 3, 2)
    return np.ascontiguousarray(words), np.ascontiguousarray(byte.astype(np.uint8).reshape(n // 512, 16, m))


K, T, S, H, C = 512, 2048, 512, 512, 512


def setup_inputs():
    n = np.random.standard_normal
    s = mx_kscale(K)[:, None]
    packed_xT = pack_weight(n((K, T)) * s)
    packed_w1 = pack_weight(n((K, H)) / np.sqrt(K) / s)
    return {
        "x_words": packed_xT[0],
        "x_scales": packed_xT[1],
        "w1_words": packed_w1[0],
        "w1_scales": packed_w1[1],
        "gs": (np.random.uniform(0.5, 1.5, (K, 1)) / s).astype(np.float32),
        "offs": striped(np.random.permutation(T)[:S]),
        "n1": striped(np.random.permutation(S)),
        "n2": striped(np.random.permutation(S)),
        "ca": striped(np.random.permutation(T)[:C]),
        "hc": striped8(np.random.randint(0, T, (8, C))),
        "n3": striped(np.random.permutation(S)),
        "n4": striped(np.random.permutation(S)),
    }


def reference(x_words, x_scales, w1_words, w1_scales, gs, offs, n1, n2, ca, hc, n3, n4):
    x_ca = unpack_weight(x_words, x_scales)[:, unstriped(ca)]
    xq = unpack_weight(x_words, x_scales)[:, unstriped(offs)]
    y = unpack_weight(w1_words, w1_scales).T @ xq
    st = y - y[:, unstriped(n1)]
    z = f64(gs) * (np.maximum(st, st[:, unstriped(n2)]))
    zq = mxq(z, 0, "e4m3")
    a = 0.0625 * (x_ca.T @ zq)
    x_hc = unpack_weight(x_words, x_scales)[np.arange(K)[:, None], runs(hc, K)]
    b = 0.0625 * (x_hc.T @ zq)
    out_0 = (a - a[:, unstriped(n3)]) / (np.abs(b) + np.abs(b[:, unstriped(n4)]) + 0.5)
    return (out_0,) + planes(out_0)

@@ -1,0 +1,290 @@
+from contextlib import ExitStack
+
+import concourse.mybir as mybir
+
+K, T, S, H, C = 512, 2048, 512, 512, 512
+FLOPS = 2 * K * H * S + 2 * 2 * K * C * S
+
+F32 = mybir.dt.float32
+BF16 = mybir.dt.bfloat16
+I32 = mybir.dt.int32
+U32 = mybir.dt.uint32
+U16 = mybir.dt.uint16
+U8 = mybir.dt.uint8
+FP8X4 = mybir.dt.float8_e4m3fn_x4
+ALU = mybir.AluOpType
+ACT = mybir.ActivationFunctionType
+
+P = 128
+PACK = 4
+LIST_ROWS = 16
+SPARE = 16
+HALF = S // 2
+OUT_CHUNKS = (256, 256)
+FUSED_ST = (0, 1)
+G2_ON_VECTOR = ()
+PLAIN_NUM = (0, 4)
+PLAIN_DEN = (0, 0)
+FETCH_AFTER = 0
+WARM = False
+HC_TAG = "slot_b"
+N2_TAG = "slot_g3"
+ST_ORDER = (0, 1, 2, 3)
+CA_EARLY = 256
+CA_TAG = "slot_g1"
+CAST_ON_SCALAR = ()
+
+
+def tile_picked_cdhnormbhopmx_none_po_kernel(
+    tc, x_words, x_scales, w1_words, w1_scales, gs, offs, n1, n2, ca, hc, n3, n4, out_0, out_1, out_2
+):
+    nc = tc.nc
+
+    with ExitStack() as ctx:
+        lists = ctx.enter_context(tc.tile_pool(name="lists", bufs=1))
+        sb = ctx.enter_context(tc.tile_pool(name="sb", bufs=1))
+        psum = ctx.enter_context(tc.psum_pool(name="psum", bufs=1))
+
+        def load_list(name, src):
+            tile = lists.tile([P, S // LIST_ROWS], U16, name=name)
+            nc.sync.dma_start(tile[:], src)
+            return tile
+
+        def entries(list_tile, start, count):
+            return list_tile[:, start // LIST_ROWS : (start + count) // LIST_ROWS]
+
+        def deal(engine, dst, src):
+            engine.tensor_copy(
+                dst[:].rearrange("p (t m) -> p t m", t=PACK),
+                src[:].rearrange("p (m t) -> p t m", t=PACK),
+            )
+
+        xs = sb.tile([P, T], U8, name="xs", align_bytes=64)
+        nc.vector.memset(xs[:].bitcast(I32), 0)
+        nc.scalar.dma_start(xs[0:P:8, :].bitcast(I32), x_scales[0].bitcast(I32))
+        w1s = sb.tile([P, H], U8, name="w1s", tag="slot_a", align_bytes=64)
+        nc.gpsimd.memset(w1s[:].bitcast(I32), 0)
+        nc.gpsimd.dma_start(w1s[0:P:8, :].bitcast(I32), w1_scales[0].bitcast(I32))
+
+        def place_scale_rows(queue, tile):
+            for r in range(1, PACK):
+                queue.dma_start(tile[r:P:32, :].bitcast(I32), tile[8 * r : P : 32, :].bitcast(I32))
+
+        gs_t = sb.tile([P, PACK], F32, name="gs_t")
+        nc.sync.dma_start(gs_t[:], gs.rearrange("(p t) o -> p (t o)", t=PACK))
+        offs_l = load_list("offs_l", offs)
+        ca_l = load_list("ca_l", ca)
+        hc_l = load_list("hc_l", hc)
+        n1_l = load_list("n1_l", n1)
+        xw = sb.tile([P, T], U32, name="xw", align_bytes=64)
+        nc.sync.dma_start(xw[:].bitcast(I32), x_words[0].rearrange("p n t -> p (n t)").bitcast(I32))
+        w1w = sb.tile([P, H], U32, name="w1w", tag="slot_b", align_bytes=64)
+        nc.sync.dma_start(w1w[:].bitcast(I32), w1_words[0].rearrange("p n t -> p (n t)").bitcast(I32))
+        n2_l = load_list("n2_l", n2)
+        n4_l = load_list("n4_l", n4)
+        n3_l = load_list("n3_l", n3)
+
+        if WARM:
+            warm = sb.tile([P, 1], F32, name="warm")
+            nc.vector.memset(warm[:], 1.0)
+            warm_out = sb.tile([P, 1], F32, name="warm_out")
+            nc.scalar.activation(warm_out[:], warm[:], ACT.Abs_reciprocal_sqrt)
+        gs_abs = sb.tile([P, PACK], F32, name="gs_abs")
+        nc.scalar.activation(gs_abs[:], gs_t[:], ACT.Abs)
+        gs_neg = sb.tile([P, PACK], F32, name="gs_neg")
+        nc.scalar.activation(gs_neg[:], gs_abs[:], ACT.Copy, scale=-1.0)
+        sgn_bf = sb.tile([P, PACK], BF16, name="sgn_bf")
+        nc.scalar.activation(sgn_bf[:], gs_t[:], ACT.Sign)
+
+        def gather_packed(name, tag, window, dtype, list_tile):
+            tile = sb.tile([P, S], dtype, name=name, tag=tag, align_bytes=64)
+            nc.vector.tensor_copy(tile[:], window[:].indirect(list_tile[:]))
+            return tile
+
+        xq_s = gather_packed("xq_s", "slot_d", xs, U8, offs_l)
+        first_scale = sb.tile([P, S + H], U8, name="first_scale", align_bytes=64)
+        nc.vector.tensor_copy(first_scale[:, :S].bitcast(I32), xq_s[:].bitcast(I32))
+        deal(nc.vector, first_scale[:, S:], w1s)
+        place_scale_rows(nc.scalar, first_scale)
+        xq_w = gather_packed("xq_w", "slot_a", xw, U32, offs_l)
+        w1w_d = sb.tile([P, H], U32, name="w1w_d", align_bytes=64)
+        deal(nc.vector, w1w_d, w1w)
+
+        cand_s = sb.tile([P, 2 * C], U8, name="cand_s", tag="slot_b", align_bytes=64)
+        nc.vector.tensor_copy(cand_s[:, :C], xs[:].indirect(ca_l[:]))
+        nc.vector.tensor_copy(cand_s[:, C:], xs[:].indirect(hc_l[:]))
+        cand_scale = sb.tile([P, 2 * C], U8, name="cand_scale", align_bytes=64)
+        nc.vector.tensor_copy(
+            cand_scale[:].rearrange("p (c t m) -> p c t m", c=2, t=PACK),
+            cand_s[:].rearrange("p (c m t) -> p c t m", c=2, t=PACK),
+        )
+        place_scale_rows(nc.gpsimd, cand_scale)
+
+        st = sb.tile([P, PACK, S], F32, name="st", align_bytes=64)
+        y_banks, us = [], []
+        for t in range(PACK):
+            cols = slice(t * P, (t + 1) * P)
+            y_ps = psum.tile([P, S], F32, name="y_ps", tag="bank%d" % t)
+            nc.tensor.matmul_mx(
+                out=y_ps[:],
+                lhsT=w1w_d[:, cols].bitcast(FP8X4),
+                lhsT_scale=first_scale[:, S + t * P : S + (t + 1) * P],
+                rhs=xq_w[:].bitcast(FP8X4),
+                rhs_scale=first_scale[:, :S],
+                start=True,
+                stop=True,
+            )
+            fused = t in FUSED_ST
+            u = sb.tile([P, S if fused else S + SPARE], F32, name="u%d" % t, align_bytes=64)
+            if not fused:
+                nc.vector.memset(u[:, S:], 0.0)
+            nc.scalar.activation(u[:, :S], y_ps[:], ACT.Copy, scale=gs_neg[:, t : t + 1])
+            y_banks.append(y_ps)
+            us.append(u)
+        for t in ST_ORDER:
+            y_ps, u = y_banks[t], us[t]
+            other = sb.tile([P, S], F32, name="other", tag="slot_g%d" % t, align_bytes=64)
+            if t in FUSED_ST:
+                nc.sync.dma_start(other[:], u[:])
+                for h in range(2):
+                    cols = slice(h * HALF, (h + 1) * HALF)
+                    nc.vector.tensor_tensor(
+                        st[:, t, cols], u[:].indirect(entries(n1_l, h * HALF, HALF)), other[:, cols], ALU.subtract
+                    )
+            else:
+                nc.scalar.activation(other[:], u[:].indirect(n1_l[:]), ACT.Copy)
+                nc.vector.scalar_tensor_tensor(
+                    st[:, t, :], y_ps[:], gs_abs[:, t : t + 1], other[:], ALU.mult, ALU.add
+                )
+
+        hc_w = gather_packed("hc_w", HC_TAG, xw, U32, hc_l)
+        hc_w_d = sb.tile([P, C], U32, name="hc_w_d", align_bytes=64)
+        deal(nc.vector, hc_w_d, hc_w)
+        ca_w_d = sb.tile([P, C], U32, name="ca_w_d", align_bytes=64)
+
+        def pick_ca_words(tag, start, count):
+            tile = sb.tile([P, count], U32, name="ca_w", tag=tag, align_bytes=64)
+            nc.vector.tensor_copy(tile[:], xw[:].indirect(entries(ca_l, start, count)))
+            nc.vector.tensor_copy(
+                ca_w_d[:].rearrange("p (t m) -> p t m", t=PACK)[:, :, start // PACK : (start + count) // PACK],
+                tile[:].rearrange("p (m t) -> p t m", t=PACK),
+            )
+
+        if CA_EARLY:
+            pick_ca_words(CA_TAG, 0, CA_EARLY)
+
+        a_win = [sb.tile([P, S], F32, name="a_win%d" % t, align_bytes=64) for t in range(PACK)]
+        b_win = [sb.tile([P, S], F32, name="b_win%d" % t, align_bytes=64) for t in range(PACK)]
+        a_own = sb.tile([P, PACK, S], F32, name="a_own", align_bytes=64)
+        b_own = sb.tile([P, PACK, S], F32, name="b_own", align_bytes=64)
+        z_w = sb.tile([P, S], U32, name="z_w", align_bytes=64)
+        z_s = sb.tile([P, S], U8, name="z_s", align_bytes=64)
+        for h in range(2):
+            cols = slice(h * HALF, (h + 1) * HALF)
+            st_n2 = sb.tile([P, PACK, HALF], F32, name="st_n2_%d" % h, tag=("st_n2", N2_TAG)[h], align_bytes=64)
+            for t in range(PACK):
+                looked_up = st[:, t, :].indirect(entries(n2_l, h * HALF, HALF))
+                if (h, t) in G2_ON_VECTOR:
+                    nc.vector.tensor_copy(st_n2[:, t, :], looked_up)
+                else:
+                    nc.scalar.activation(st_n2[:, t, :], looked_up, ACT.Copy)
+            z_abs = sb.tile([P, HALF * PACK], BF16, name="z_abs", align_bytes=64)
+            nc.vector.tensor_tensor(
+                z_abs[:].rearrange("p (c i t) -> p c t i", i=4, t=PACK),
+                st[:, :, cols].rearrange("p t (c i) -> p c t i", i=4),
+                st_n2[:].rearrange("p t (c i) -> p c t i", i=4),
+                ALU.max,
+            )
+            z_bf = sb.tile([P, HALF * PACK], BF16, name="z_bf", tag="slot_z%d" % h, align_bytes=64)
+            nc.vector.tensor_tensor(
+                z_bf[:].rearrange("p (j t) -> p j t", t=PACK),
+                z_abs[:].rearrange("p (j t) -> p j t", t=PACK),
+                sgn_bf[:].unsqueeze(1).to_broadcast([P, HALF, PACK]),
+                ALU.mult,
+            )
+            nc.vector.quantize_mx(out=z_w[:, cols].bitcast(FP8X4), scales=z_s[:, cols], in_=z_bf[:])
+            for t in range(PACK):
+                rows = slice(t * P, (t + 1) * P)
+                b_ps = psum.tile([P, HALF], F32, name="b_ps", tag="bank%d" % (PACK + (t + 2 * h) % PACK))
+                nc.tensor.matmul_mx(
+                    out=b_ps[:],
+                    lhsT=hc_w_d[:, rows].bitcast(FP8X4),
+                    lhsT_scale=cand_scale[:, C + t * P : C + (t + 1) * P],
+                    rhs=z_w[:, cols].bitcast(FP8X4),
+                    rhs_scale=z_s[:, cols],
+                    start=True,
+                    stop=True,
+                )
+                nc.scalar.activation(b_win[t][:, cols], b_ps[:], ACT.Abs)
+                nc.sync.dma_start(b_own[:, t, cols], b_win[t][:, cols])
+
+        if CA_EARLY < C:
+            pick_ca_words("slot_z1", CA_EARLY, C - CA_EARLY)
+        for t in range(PACK):
+            rows = slice(t * P, (t + 1) * P)
+            a_ps = psum.tile([P, S], F32, name="a_ps", tag="bank%d" % t)
+            nc.tensor.matmul_mx(
+                out=a_ps[:],
+                lhsT=ca_w_d[:, rows].bitcast(FP8X4),
+                lhsT_scale=cand_scale[:, rows],
+                rhs=z_w[:].bitcast(FP8X4),
+                rhs_scale=z_s[:],
+                start=True,
+                stop=True,
+            )
+            nc.scalar.activation(a_win[t][:], a_ps[:], ACT.Copy, scale=-1.0)
+            nc.sync.dma_start(a_own[:, t, :], a_win[t][:])
+
+        out_rows = out_0.rearrange("(p t) j -> p t j", t=PACK)
+        words_out = out_1[0].rearrange("p n t -> p (n t)").bitcast(I32)
+        o_s = sb.tile([P, S], U8, name="o_s", align_bytes=64)
+        def combine(dst, win, own, got, list_tile, op, plain, c, start, width):
+            cols = slice(start, start + width)
+            for t in range(PACK - plain[c]):
+                nc.vector.tensor_tensor(dst[:, t, :], win[t][:].indirect(entries(list_tile, start, width)), own[:, t, cols], op)
+            if plain[c]:
+                rest = slice(PACK - plain[c], PACK)
+                nc.vector.tensor_tensor(dst[:, rest, :], got[:, rest, cols], own[:, rest, cols], op)
+
+        def fetch(win, got, list_tile, plain, c, start, width):
+            for t in range(PACK - plain[c], PACK):
+                nc.scalar.activation(got[:, t, start : start + width], win[t][:].indirect(entries(list_tile, start, width)), ACT.Copy)
+
+        starts = [sum(OUT_CHUNKS[:c]) for c in range(len(OUT_CHUNKS))]
+        a_got = sb.tile([P, PACK, S], F32, name="a_got", align_bytes=64)
+        b_got = sb.tile([P, PACK, S], F32, name="b_got", align_bytes=64) if any(PLAIN_DEN) else None
+        for c, (start, width) in enumerate(zip(starts, OUT_CHUNKS)):
+            fetch(b_win, b_got, n4_l, PLAIN_DEN, c, start, width)
+        recips = []
+        for c, (start, width) in enumerate(zip(starts, OUT_CHUNKS)):
+            den = sb.tile([P, PACK, width], F32, name="den%d" % c, align_bytes=64)
+            combine(den, b_win, b_own, b_got, n4_l, ALU.add, PLAIN_DEN, c, start, width)
+            root = sb.tile([P, PACK, width], F32, name="root%d" % c, align_bytes=64)
+            nc.scalar.activation(root[:], den[:], ACT.Abs_reciprocal_sqrt, bias=8.0)
+            recip = sb.tile([P, PACK, width], F32, name="recip%d" % c, align_bytes=64)
+            nc.scalar.activation(recip[:], root[:], ACT.Square)
+            recips.append(recip)
+            if c == FETCH_AFTER:
+                for c2, (start2, width2) in enumerate(zip(starts, OUT_CHUNKS)):
+                    fetch(a_win, a_got, n3_l, PLAIN_NUM, c2, start2, width2)
+        for c, (start, width) in enumerate(zip(starts, OUT_CHUNKS)):
+            cols = slice(start, start + width)
+            recip = recips[c]
+            num = sb.tile([P, PACK, width], F32, name="num%d" % c, align_bytes=64)
+            combine(num, a_win, a_own, a_got, n3_l, ALU.subtract, PLAIN_NUM, c, start, width)
+            res = sb.tile([P, PACK * width], F32, name="res%d" % c, align_bytes=64)
+            nc.vector.tensor_tensor(
+                res[:], num[:].rearrange("p t j -> p (t j)"), recip[:].rearrange("p t j -> p (t j)"), ALU.mult
+            )
+            nc.sync.dma_start(out_rows[:, :, cols], res[:].rearrange("p (t j) -> p t j", t=PACK))
+            res_bf = sb.tile([P, width * PACK], BF16, name="res_bf%d" % c, align_bytes=64)
+            (nc.scalar.copy if c in CAST_ON_SCALAR else nc.vector.tensor_copy)(
+                res_bf[:].rearrange("p (c i t) -> p c t i", i=4, t=PACK),
+                res[:].rearrange("p (t c i) -> p c t i", i=4, t=PACK),
+            )
+            o_w = sb.tile([P, width], U32, name="o_w%d" % c, align_bytes=64)
+            nc.vector.quantize_mx(out=o_w[:].bitcast(FP8X4), scales=o_s[:, cols], in_=res_bf[:])
+            nc.scalar.dma_start(words_out[:, cols], o_w[:].bitcast(I32))
+        for r in range(PACK):
+            queue = nc.sync if r % 2 == 0 else nc.scalar
+            queue.dma_start(out_2[0, r:16:PACK, :].bitcast(I32), o_s[r:P:32, :].bitcast(I32))

@@ -20,19 +20,15 @@ PACK = 4
 LIST_ROWS = 16
 SPARE = 16
 HALF = S // 2
-OUT_CHUNKS = (256, 256)
+QUARTER = S // 4
 FUSED_ST = (0, 1)
-G2_ON_VECTOR = ()
-PLAIN_NUM = (0, 4)
-PLAIN_DEN = (0, 0)
-FETCH_AFTER = 0
-WARM = False
-HC_TAG = "slot_b"
-N2_TAG = "slot_g3"
+G2_ON_VECTOR = ((0, 3),)
+WARM = True
+Y_PARTS = 1
+STT = False
+EVAC_ORDER = ((0, 0), (0, 1), (1, 0), (1, 1), (0, 2), (1, 2), (0, 3), (1, 3))
+OWN_BY_SCALAR = 2
 ST_ORDER = (0, 1, 2, 3)
-CA_EARLY = 256
-CA_TAG = "slot_g1"
-CAST_ON_SCALAR = ()
 
 
 def tile_picked_cdhnormbhopmx_none_po_kernel(
@@ -43,6 +39,7 @@ def tile_picked_cdhnormbhopmx_none_po_kernel(
     with ExitStack() as ctx:
         lists = ctx.enter_context(tc.tile_pool(name="lists", bufs=1))
         sb = ctx.enter_context(tc.tile_pool(name="sb", bufs=1))
+        reuse = ctx.enter_context(tc.tile_pool(name="reuse", bufs=1))
         psum = ctx.enter_context(tc.psum_pool(name="psum", bufs=1))
 
         def load_list(name, src):
@@ -53,6 +50,12 @@ def tile_picked_cdhnormbhopmx_none_po_kernel(
         def entries(list_tile, start, count):
             return list_tile[:, start // LIST_ROWS : (start + count) // LIST_ROWS]
 
+        def deal_words(dst, src):
+            nc.vector.tensor_copy(
+                dst.rearrange("p t (c i) -> p c t i", i=4),
+                src.rearrange("p (c i t) -> p c t i", i=4, t=PACK),
+            )
+
         def deal(engine, dst, src):
             engine.tensor_copy(
                 dst[:].rearrange("p (t m) -> p t m", t=PACK),
@@ -61,10 +64,10 @@ def tile_picked_cdhnormbhopmx_none_po_kernel(
 
         xs = sb.tile([P, T], U8, name="xs", align_bytes=64)
         nc.vector.memset(xs[:].bitcast(I32), 0)
-        nc.scalar.dma_start(xs[0:P:8, :].bitcast(I32), x_scales[0].bitcast(I32))
-        w1s = sb.tile([P, H], U8, name="w1s", tag="slot_a", align_bytes=64)
+        nc.sync.dma_start(xs[0:P:8, :].bitcast(I32), x_scales[0].bitcast(I32))
+        w1s = sb.tile([P, H], U8, name="w1s", align_bytes=64)
         nc.gpsimd.memset(w1s[:].bitcast(I32), 0)
-        nc.gpsimd.dma_start(w1s[0:P:8, :].bitcast(I32), w1_scales[0].bitcast(I32))
+        nc.sync.dma_start(w1s[0:P:8, :].bitcast(I32), w1_scales[0].bitcast(I32))
 
         def place_scale_rows(queue, tile):
             for r in range(1, PACK):
@@ -74,12 +77,12 @@ def tile_picked_cdhnormbhopmx_none_po_kernel(
         nc.sync.dma_start(gs_t[:], gs.rearrange("(p t) o -> p (t o)", t=PACK))
         offs_l = load_list("offs_l", offs)
         ca_l = load_list("ca_l", ca)
-        hc_l = load_list("hc_l", hc)
         n1_l = load_list("n1_l", n1)
+        w1w = sb.tile([P, H], U32, name="w1w", align_bytes=64)
+        nc.sync.dma_start(w1w[:].bitcast(I32), w1_words[0].rearrange("p n t -> p (n t)").bitcast(I32))
         xw = sb.tile([P, T], U32, name="xw", align_bytes=64)
         nc.sync.dma_start(xw[:].bitcast(I32), x_words[0].rearrange("p n t -> p (n t)").bitcast(I32))
-        w1w = sb.tile([P, H], U32, name="w1w", tag="slot_b", align_bytes=64)
-        nc.sync.dma_start(w1w[:].bitcast(I32), w1_words[0].rearrange("p n t -> p (n t)").bitcast(I32))
+        hc_l = load_list("hc_l", hc)
         n2_l = load_list("n2_l", n2)
         n4_l = load_list("n4_l", n4)
         n3_l = load_list("n3_l", n3)
@@ -96,82 +99,84 @@ def tile_picked_cdhnormbhopmx_none_po_kernel(
         sgn_bf = sb.tile([P, PACK], BF16, name="sgn_bf")
         nc.scalar.activation(sgn_bf[:], gs_t[:], ACT.Sign)
 
-        def gather_packed(name, tag, window, dtype, list_tile):
-            tile = sb.tile([P, S], dtype, name=name, tag=tag, align_bytes=64)
-            nc.vector.tensor_copy(tile[:], window[:].indirect(list_tile[:]))
-            return tile
-
-        xq_s = gather_packed("xq_s", "slot_d", xs, U8, offs_l)
+        picked_s = sb.tile([P, 2 * C], U8, name="picked_s", align_bytes=64)
+        xq_s = picked_s[:, HALF : HALF + S]
+        nc.vector.tensor_copy(xq_s, xs[:].indirect(offs_l[:]))
         first_scale = sb.tile([P, S + H], U8, name="first_scale", align_bytes=64)
-        nc.vector.tensor_copy(first_scale[:, :S].bitcast(I32), xq_s[:].bitcast(I32))
         deal(nc.vector, first_scale[:, S:], w1s)
+        nc.vector.tensor_copy(picked_s[:, :HALF], xs[:].indirect(entries(ca_l, 0, HALF)))
+        nc.vector.tensor_copy(first_scale[:, :S].bitcast(I32), xq_s.bitcast(I32))
         place_scale_rows(nc.scalar, first_scale)
-        xq_w = gather_packed("xq_w", "slot_a", xw, U32, offs_l)
         w1w_d = sb.tile([P, H], U32, name="w1w_d", align_bytes=64)
-        deal(nc.vector, w1w_d, w1w)
+        deal_words(w1w_d[:].rearrange("p (t m) -> p t m", t=PACK), w1w[:])
+        nc.vector.tensor_copy(picked_s[:, HALF:C], xs[:].indirect(entries(ca_l, HALF, HALF)))
+        xq_w = sb.tile([P, S], U32, name="xq_w", align_bytes=64)
+        nc.vector.tensor_copy(xq_w[:], xw[:].indirect(offs_l[:]))
 
-        cand_s = sb.tile([P, 2 * C], U8, name="cand_s", tag="slot_b", align_bytes=64)
-        nc.vector.tensor_copy(cand_s[:, :C], xs[:].indirect(ca_l[:]))
-        nc.vector.tensor_copy(cand_s[:, C:], xs[:].indirect(hc_l[:]))
+        nc.vector.tensor_copy(picked_s[:, C:], xs[:].indirect(hc_l[:]))
+        hc_w = sb.tile([P, C], U32, name="hc_w", align_bytes=64)
+        nc.vector.tensor_copy(hc_w[:], xw[:].indirect(hc_l[:]))
         cand_scale = sb.tile([P, 2 * C], U8, name="cand_scale", align_bytes=64)
         nc.vector.tensor_copy(
             cand_scale[:].rearrange("p (c t m) -> p c t m", c=2, t=PACK),
-            cand_s[:].rearrange("p (c m t) -> p c t m", c=2, t=PACK),
+            picked_s[:].rearrange("p (c m t) -> p c t m", c=2, t=PACK),
         )
         place_scale_rows(nc.gpsimd, cand_scale)
+        ca_w0 = sb.tile([P, HALF], U32, name="ca_w0", align_bytes=64)
+        nc.vector.tensor_copy(ca_w0[:], xw[:].indirect(entries(ca_l, 0, HALF)))
+        hc_w_d = sb.tile([P, C], U32, name="hc_w_d", align_bytes=64)
+        deal_words(hc_w_d[:].rearrange("p (t m) -> p t m", t=PACK), hc_w[:])
+        ca_w_d = sb.tile([P, PACK, P], U32, name="ca_w_d", align_bytes=64)
+        deal_words(ca_w_d[:, :, : P // 2], ca_w0[:])
 
-        st = sb.tile([P, PACK, S], F32, name="st", align_bytes=64)
-        y_banks, us = [], []
+        st = sb.tile([P, PACK, S + HALF], F32, name="st", align_bytes=64)
+        us = []
         for t in range(PACK):
-            cols = slice(t * P, (t + 1) * P)
-            y_ps = psum.tile([P, S], F32, name="y_ps", tag="bank%d" % t)
-            nc.tensor.matmul_mx(
-                out=y_ps[:],
-                lhsT=w1w_d[:, cols].bitcast(FP8X4),
-                lhsT_scale=first_scale[:, S + t * P : S + (t + 1) * P],
-                rhs=xq_w[:].bitcast(FP8X4),
-                rhs_scale=first_scale[:, :S],
-                start=True,
-                stop=True,
-            )
-            fused = t in FUSED_ST
-            u = sb.tile([P, S if fused else S + SPARE], F32, name="u%d" % t, align_bytes=64)
-            if not fused:
+            spare = 0 if t in FUSED_ST else SPARE
+            u = sb.tile([P, S + spare], F32, name="u%d" % t, align_bytes=64)
+            if spare:
                 nc.vector.memset(u[:, S:], 0.0)
-            nc.scalar.activation(u[:, :S], y_ps[:], ACT.Copy, scale=gs_neg[:, t : t + 1])
-            y_banks.append(y_ps)
             us.append(u)
+        y_banks = {}
+        y_width = S // Y_PARTS
+        for h in range(Y_PARTS):
+            cols = slice(h * y_width, (h + 1) * y_width)
+            for t in range(PACK):
+                y_ps = psum.tile([P, y_width], F32, name="y_ps", tag="bank%d" % (PACK * h + t))
+                nc.tensor.matmul_mx(
+                    out=y_ps[:],
+                    lhsT=w1w_d[:, t * P : (t + 1) * P].bitcast(FP8X4),
+                    lhsT_scale=first_scale[:, S + t * P : S + (t + 1) * P],
+                    rhs=xq_w[:, cols].bitcast(FP8X4),
+                    rhs_scale=first_scale[:, cols],
+                    start=True,
+                    stop=True,
+                )
+                y_banks[h, t] = y_ps
+        for h, t in EVAC_ORDER:
+            if h < Y_PARTS:
+                nc.scalar.activation(us[t][:, h * y_width : (h + 1) * y_width], y_banks[h, t][:], ACT.Copy, scale=gs_neg[:, t : t + 1])
         for t in ST_ORDER:
-            y_ps, u = y_banks[t], us[t]
-            other = sb.tile([P, S], F32, name="other", tag="slot_g%d" % t, align_bytes=64)
+            u = us[t]
             if t in FUSED_ST:
-                nc.sync.dma_start(other[:], u[:])
+                other = st[:, t + 2, HALF:]
                 for h in range(2):
                     cols = slice(h * HALF, (h + 1) * HALF)
+                    nc.sync.dma_start(other[:, cols], u[:, cols])
                     nc.vector.tensor_tensor(
                         st[:, t, cols], u[:].indirect(entries(n1_l, h * HALF, HALF)), other[:, cols], ALU.subtract
                     )
             else:
+                other = reuse.tile([P, S], F32, name="other%d" % t, offset=4096 + 5120 * (t - 2), align_bytes=64)
                 nc.scalar.activation(other[:], u[:].indirect(n1_l[:]), ACT.Copy)
-                nc.vector.scalar_tensor_tensor(
-                    st[:, t, :], y_ps[:], gs_abs[:, t : t + 1], other[:], ALU.mult, ALU.add
-                )
-
-        hc_w = gather_packed("hc_w", HC_TAG, xw, U32, hc_l)
-        hc_w_d = sb.tile([P, C], U32, name="hc_w_d", align_bytes=64)
-        deal(nc.vector, hc_w_d, hc_w)
-        ca_w_d = sb.tile([P, C], U32, name="ca_w_d", align_bytes=64)
-
-        def pick_ca_words(tag, start, count):
-            tile = sb.tile([P, count], U32, name="ca_w", tag=tag, align_bytes=64)
-            nc.vector.tensor_copy(tile[:], xw[:].indirect(entries(ca_l, start, count)))
-            nc.vector.tensor_copy(
-                ca_w_d[:].rearrange("p (t m) -> p t m", t=PACK)[:, :, start // PACK : (start + count) // PACK],
-                tile[:].rearrange("p (m t) -> p t m", t=PACK),
-            )
-
-        if CA_EARLY:
-            pick_ca_words(CA_TAG, 0, CA_EARLY)
+                if STT:
+                    for h in range(2):
+                        cols = slice(h * HALF, (h + 1) * HALF)
+                        nc.vector.scalar_tensor_tensor(
+                            st[:, t, cols], y_banks[h, t][:], gs_abs[:, t : t + 1], other[:, cols], ALU.mult, ALU.add
+                        )
+                else:
+                    nc.vector.tensor_tensor(st[:, t, :S], other[:], u[:, :S], ALU.subtract)
 
         a_win = [sb.tile([P, S], F32, name="a_win%d" % t, align_bytes=64) for t in range(PACK)]
         b_win = [sb.tile([P, S], F32, name="b_win%d" % t, align_bytes=64) for t in range(PACK)]
@@ -181,28 +186,36 @@ def tile_picked_cdhnormbhopmx_none_po_kernel(
         z_s = sb.tile([P, S], U8, name="z_s", align_bytes=64)
         for h in range(2):
             cols = slice(h * HALF, (h + 1) * HALF)
-            st_n2 = sb.tile([P, PACK, HALF], F32, name="st_n2_%d" % h, tag=("st_n2", N2_TAG)[h], align_bytes=64)
+            st_n2 = reuse.tile([P, PACK, HALF], F32, name="st_n2_%d" % h, offset=(0, 9216)[h], align_bytes=64)
             for t in range(PACK):
-                looked_up = st[:, t, :].indirect(entries(n2_l, h * HALF, HALF))
+                looked_up = st[:, t, :S].indirect(entries(n2_l, h * HALF, HALF))
                 if (h, t) in G2_ON_VECTOR:
                     nc.vector.tensor_copy(st_n2[:, t, :], looked_up)
                 else:
                     nc.scalar.activation(st_n2[:, t, :], looked_up, ACT.Copy)
-            z_abs = sb.tile([P, HALF * PACK], BF16, name="z_abs", align_bytes=64)
-            nc.vector.tensor_tensor(
-                z_abs[:].rearrange("p (c i t) -> p c t i", i=4, t=PACK),
-                st[:, :, cols].rearrange("p t (c i) -> p c t i", i=4),
-                st_n2[:].rearrange("p t (c i) -> p c t i", i=4),
-                ALU.max,
-            )
-            z_bf = sb.tile([P, HALF * PACK], BF16, name="z_bf", tag="slot_z%d" % h, align_bytes=64)
-            nc.vector.tensor_tensor(
-                z_bf[:].rearrange("p (j t) -> p j t", t=PACK),
-                z_abs[:].rearrange("p (j t) -> p j t", t=PACK),
-                sgn_bf[:].unsqueeze(1).to_broadcast([P, HALF, PACK]),
-                ALU.mult,
-            )
-            nc.vector.quantize_mx(out=z_w[:, cols].bitcast(FP8X4), scales=z_s[:, cols], in_=z_bf[:])
+            parts = [slice(h * HALF + e * QUARTER, h * HALF + (e + 1) * QUARTER) for e in range(2)]
+            z_abs = [sb.tile([P, QUARTER * PACK], BF16, name="z_abs%d" % e, align_bytes=64) for e in range(2)]
+            z_bf = [
+                sb.tile([P, QUARTER * PACK], BF16, name="z_bf", tag="slot_z%d%d" % (h, e), align_bytes=64)
+                for e in range(2)
+            ]
+            for e, part in enumerate(parts):
+                nc.vector.tensor_tensor(
+                    z_abs[e][:].rearrange("p (c i t) -> p c t i", i=4, t=PACK),
+                    st[:, :, part].rearrange("p t (c i) -> p c t i", i=4),
+                    st_n2[:, :, e * QUARTER : (e + 1) * QUARTER].rearrange("p t (c i) -> p c t i", i=4),
+                    ALU.max,
+                )
+            for e in range(2):
+                nc.vector.tensor_tensor(
+                    z_bf[e][:].rearrange("p (j t) -> p j t", t=PACK),
+                    z_abs[e][:].rearrange("p (j t) -> p j t", t=PACK),
+                    sgn_bf[:].unsqueeze(1).to_broadcast([P, QUARTER, PACK]),
+                    ALU.mult,
+                )
+            for e, part in enumerate(parts):
+                nc.vector.quantize_mx(out=z_w[:, part].bitcast(FP8X4), scales=z_s[:, part], in_=z_bf[e][:])
+            twice = []
             for t in range(PACK):
                 rows = slice(t * P, (t + 1) * P)
                 b_ps = psum.tile([P, HALF], F32, name="b_ps", tag="bank%d" % (PACK + (t + 2 * h) % PACK))
@@ -216,16 +229,22 @@ def tile_picked_cdhnormbhopmx_none_po_kernel(
                     stop=True,
                 )
                 nc.scalar.activation(b_win[t][:, cols], b_ps[:], ACT.Abs)
-                nc.sync.dma_start(b_own[:, t, cols], b_win[t][:, cols])
+                if h == 0 and t < OWN_BY_SCALAR:
+                    twice.append((t, b_ps))
+                else:
+                    nc.sync.dma_start(b_own[:, t, cols], b_win[t][:, cols])
+            for t, b_ps in twice:
+                nc.scalar.activation(b_own[:, t, cols], b_ps[:], ACT.Abs)
 
-        if CA_EARLY < C:
-            pick_ca_words("slot_z1", CA_EARLY, C - CA_EARLY)
+        ca_w1 = sb.tile([P, HALF], U32, name="ca_w1", tag="slot_z10", align_bytes=64)
+        nc.vector.tensor_copy(ca_w1[:], xw[:].indirect(entries(ca_l, HALF, HALF)))
+        deal_words(ca_w_d[:, :, P // 2 :], ca_w1[:])
         for t in range(PACK):
             rows = slice(t * P, (t + 1) * P)
             a_ps = psum.tile([P, S], F32, name="a_ps", tag="bank%d" % t)
             nc.tensor.matmul_mx(
                 out=a_ps[:],
-                lhsT=ca_w_d[:, rows].bitcast(FP8X4),
+                lhsT=ca_w_d[:, t, :].bitcast(FP8X4),
                 lhsT_scale=cand_scale[:, rows],
                 rhs=z_w[:].bitcast(FP8X4),
                 rhs_scale=z_s[:],
@@ -238,53 +257,73 @@ def tile_picked_cdhnormbhopmx_none_po_kernel(
         out_rows = out_0.rearrange("(p t) j -> p t j", t=PACK)
         words_out = out_1[0].rearrange("p n t -> p (n t)").bitcast(I32)
         o_s = sb.tile([P, S], U8, name="o_s", align_bytes=64)
-        def combine(dst, win, own, got, list_tile, op, plain, c, start, width):
-            cols = slice(start, start + width)
-            for t in range(PACK - plain[c]):
-                nc.vector.tensor_tensor(dst[:, t, :], win[t][:].indirect(entries(list_tile, start, width)), own[:, t, cols], op)
-            if plain[c]:
-                rest = slice(PACK - plain[c], PACK)
-                nc.vector.tensor_tensor(dst[:, rest, :], got[:, rest, cols], own[:, rest, cols], op)
+        first, second = slice(0, HALF), slice(HALF, S)
+        quarters = [slice(HALF + e * QUARTER, HALF + (e + 1) * QUARTER) for e in range(2)]
 
-        def fetch(win, got, list_tile, plain, c, start, width):
-            for t in range(PACK - plain[c], PACK):
-                nc.scalar.activation(got[:, t, start : start + width], win[t][:].indirect(entries(list_tile, start, width)), ACT.Copy)
+        den = sb.tile([P, PACK, S], F32, name="den", align_bytes=64)
+        for h, cols in enumerate((first, second)):
+            for t in range(PACK):
+                nc.vector.tensor_tensor(
+                    den[:, t, cols], b_win[t][:].indirect(entries(n4_l, h * HALF, HALF)), b_own[:, t, cols], ALU.add
+                )
+        root = sb.tile([P, PACK, S], F32, name="root", align_bytes=64)
+        recip = sb.tile([P, PACK, S], F32, name="recip", align_bytes=64)
+        a_got = sb.tile([P, PACK, HALF], F32, name="a_got", align_bytes=64)
 
-        starts = [sum(OUT_CHUNKS[:c]) for c in range(len(OUT_CHUNKS))]
-        a_got = sb.tile([P, PACK, S], F32, name="a_got", align_bytes=64)
-        b_got = sb.tile([P, PACK, S], F32, name="b_got", align_bytes=64) if any(PLAIN_DEN) else None
-        for c, (start, width) in enumerate(zip(starts, OUT_CHUNKS)):
-            fetch(b_win, b_got, n4_l, PLAIN_DEN, c, start, width)
-        recips = []
-        for c, (start, width) in enumerate(zip(starts, OUT_CHUNKS)):
-            den = sb.tile([P, PACK, width], F32, name="den%d" % c, align_bytes=64)
-            combine(den, b_win, b_own, b_got, n4_l, ALU.add, PLAIN_DEN, c, start, width)
-            root = sb.tile([P, PACK, width], F32, name="root%d" % c, align_bytes=64)
-            nc.scalar.activation(root[:], den[:], ACT.Abs_reciprocal_sqrt, bias=8.0)
-            recip = sb.tile([P, PACK, width], F32, name="recip%d" % c, align_bytes=64)
-            nc.scalar.activation(recip[:], root[:], ACT.Square)
-            recips.append(recip)
-            if c == FETCH_AFTER:
-                for c2, (start2, width2) in enumerate(zip(starts, OUT_CHUNKS)):
-                    fetch(a_win, a_got, n3_l, PLAIN_NUM, c2, start2, width2)
-        for c, (start, width) in enumerate(zip(starts, OUT_CHUNKS)):
-            cols = slice(start, start + width)
-            recip = recips[c]
-            num = sb.tile([P, PACK, width], F32, name="num%d" % c, align_bytes=64)
-            combine(num, a_win, a_own, a_got, n3_l, ALU.subtract, PLAIN_NUM, c, start, width)
-            res = sb.tile([P, PACK * width], F32, name="res%d" % c, align_bytes=64)
-            nc.vector.tensor_tensor(
-                res[:], num[:].rearrange("p t j -> p (t j)"), recip[:].rearrange("p t j -> p (t j)"), ALU.mult
-            )
-            nc.sync.dma_start(out_rows[:, :, cols], res[:].rearrange("p (t j) -> p t j", t=PACK))
-            res_bf = sb.tile([P, width * PACK], BF16, name="res_bf%d" % c, align_bytes=64)
-            (nc.scalar.copy if c in CAST_ON_SCALAR else nc.vector.tensor_copy)(
+        def fetch(t):
+            nc.scalar.activation(a_got[:, t, :], a_win[t][:].indirect(entries(n3_l, HALF, HALF)), ACT.Copy)
+
+        nc.scalar.activation(root[:, :, first], den[:, :, first], ACT.Abs_reciprocal_sqrt, bias=8.0)
+        fetch(0)
+        nc.scalar.activation(recip[:, :, first], root[:, :, first], ACT.Square)
+        for t in range(1, PACK):
+            fetch(t)
+        for cols in quarters:
+            nc.scalar.activation(root[:, :, cols], den[:, :, cols], ACT.Abs_reciprocal_sqrt, bias=8.0)
+        for cols in quarters:
+            nc.scalar.activation(recip[:, :, cols], root[:, :, cols], ACT.Square)
+
+        res = sb.tile([P, PACK, S], F32, name="res", align_bytes=64)
+        num = sb.tile([P, PACK, HALF], F32, name="num", align_bytes=64)
+        for t in range(PACK):
+            width = QUARTER if t == PACK - 1 else HALF
+            for start in range(0, HALF, width):
+                cols = slice(start, start + width)
+                nc.vector.tensor_tensor(
+                    num[:, t, cols], a_win[t][:].indirect(entries(n3_l, start, width)), a_own[:, t, cols], ALU.subtract
+                )
+        for e in range(2):
+            cols = slice(e * QUARTER, (e + 1) * QUARTER)
+            nc.vector.tensor_tensor(res[:, :, cols], num[:, :, cols], recip[:, :, cols], ALU.mult)
+        nc.sync.dma_start(out_rows[:, :, first], res[:, :, first])
+
+        def round_and_pack(copy, cols, name):
+            width = cols.stop - cols.start
+            res_bf = sb.tile([P, width * PACK], BF16, name=name, align_bytes=64)
+            copy(
                 res_bf[:].rearrange("p (c i t) -> p c t i", i=4, t=PACK),
-                res[:].rearrange("p (t c i) -> p c t i", i=4, t=PACK),
+                res[:, :, cols].rearrange("p t (c i) -> p c t i", i=4),
             )
-            o_w = sb.tile([P, width], U32, name="o_w%d" % c, align_bytes=64)
-            nc.vector.quantize_mx(out=o_w[:].bitcast(FP8X4), scales=o_s[:, cols], in_=res_bf[:])
-            nc.scalar.dma_start(words_out[:, cols], o_w[:].bitcast(I32))
+            return res_bf
+
+        o_w = sb.tile([P, S], U32, name="o_w", align_bytes=64)
+
+        def quantise(cols, res_bf):
+            nc.vector.quantize_mx(out=o_w[:, cols].bitcast(FP8X4), scales=o_s[:, cols], in_=res_bf[:])
+
+        first_bf = round_and_pack(nc.scalar.copy, first, "first_bf")
+        for e, cols in enumerate(quarters):
+            part = slice(e * QUARTER, (e + 1) * QUARTER)
+            nc.vector.tensor_tensor(num[:, :, part], a_got[:, :, part], a_own[:, :, cols], ALU.subtract)
+        for e, cols in enumerate(quarters):
+            nc.vector.tensor_tensor(res[:, :, cols], num[:, :, e * QUARTER : (e + 1) * QUARTER], recip[:, :, cols], ALU.mult)
+            nc.sync.dma_start(out_rows[:, :, cols], res[:, :, cols])
+        late_bf = [round_and_pack(nc.vector.tensor_copy, cols, "late_bf%d" % e) for e, cols in enumerate(quarters)]
+        quantise(quarters[0], late_bf[0])
+        quantise(first, first_bf)
+        quantise(quarters[1], late_bf[1])
+        nc.scalar.dma_start(words_out[:, : S - QUARTER], o_w[:, : S - QUARTER].bitcast(I32))
+        nc.sync.dma_start(words_out[:, S - QUARTER :], o_w[:, S - QUARTER :].bitcast(I32))
         for r in range(PACK):
             queue = nc.sync if r % 2 == 0 else nc.scalar
             queue.dma_start(out_2[0, r:16:PACK, :].bitcast(I32), o_s[r:P:32, :].bitcast(I32))

@@ -21,14 +21,12 @@ LIST_ROWS = 16
 SPARE = 16
 HALF = S // 2
 QUARTER = S // 4
-FUSED_ST = (0, 1)
-G2_ON_VECTOR = ((0, 3),)
+G2_PLAN = (((0,1,0,256),(0,2,0,256),(1,0,0,256),(0,3,0,128),(0,3,128,128)), ((0,0,0,128),(0,1,0,128),(0,2,0,128),(0,3,0,128),(0,0,128,128),(0,1,128,128),(0,2,128,128),(0,3,128,128)))
 WARM = True
-Y_PARTS = 1
-STT = False
-EVAC_ORDER = ((0, 0), (0, 1), (1, 0), (1, 1), (0, 2), (1, 2), (0, 3), (1, 3))
+OWN0 = "S"
+DUP1 = "S"
+CLOCK = False
 OWN_BY_SCALAR = 2
-ST_ORDER = (0, 1, 2, 3)
 
 
 def tile_picked_cdhnormbhopmx_none_po_kernel(
@@ -121,63 +119,56 @@ def tile_picked_cdhnormbhopmx_none_po_kernel(
             cand_scale[:].rearrange("p (c t m) -> p c t m", c=2, t=PACK),
             picked_s[:].rearrange("p (c m t) -> p c t m", c=2, t=PACK),
         )
-        place_scale_rows(nc.gpsimd, cand_scale)
+        place_scale_rows(nc.sync, cand_scale)
         ca_w0 = sb.tile([P, HALF], U32, name="ca_w0", align_bytes=64)
         nc.vector.tensor_copy(ca_w0[:], xw[:].indirect(entries(ca_l, 0, HALF)))
-        hc_w_d = sb.tile([P, C], U32, name="hc_w_d", align_bytes=64)
-        deal_words(hc_w_d[:].rearrange("p (t m) -> p t m", t=PACK), hc_w[:])
-        ca_w_d = sb.tile([P, PACK, P], U32, name="ca_w_d", align_bytes=64)
-        deal_words(ca_w_d[:, :, : P // 2], ca_w0[:])
 
         st = sb.tile([P, PACK, S + HALF], F32, name="st", align_bytes=64)
         us = []
         for t in range(PACK):
-            spare = 0 if t in FUSED_ST else SPARE
+            y_ps = psum.tile([P, S], F32, name="y_ps", tag="bank%d" % t)
+            nc.tensor.matmul_mx(
+                out=y_ps[:],
+                lhsT=w1w_d[:, t * P : (t + 1) * P].bitcast(FP8X4),
+                lhsT_scale=first_scale[:, S + t * P : S + (t + 1) * P],
+                rhs=xq_w[:].bitcast(FP8X4),
+                rhs_scale=first_scale[:, :S],
+                start=True,
+                stop=True,
+            )
+            spare = 0 if t < 2 else SPARE
             u = sb.tile([P, S + spare], F32, name="u%d" % t, align_bytes=64)
             if spare:
                 nc.vector.memset(u[:, S:], 0.0)
+            nc.scalar.activation(u[:, :S], y_ps[:], ACT.Copy, scale=gs_neg[:, t : t + 1])
+            if t == 0:
+                (nc.scalar if DUP1 == "S" else nc.sync).dma_start(st[:, 3, HALF:], u[:])
+            if t == 1 and OWN0 == "V":
+                nc.vector.tensor_scalar(st[:, 2, HALF:], y_ps[:], gs_neg[:, t : t + 1], None, ALU.mult)
+            if t == 1 and OWN0 == "S":
+                nc.scalar.activation(st[:, 2, HALF:], y_ps[:], ACT.Copy, scale=gs_neg[:, t : t + 1])
             us.append(u)
-        y_banks = {}
-        y_width = S // Y_PARTS
-        for h in range(Y_PARTS):
-            cols = slice(h * y_width, (h + 1) * y_width)
-            for t in range(PACK):
-                y_ps = psum.tile([P, y_width], F32, name="y_ps", tag="bank%d" % (PACK * h + t))
-                nc.tensor.matmul_mx(
-                    out=y_ps[:],
-                    lhsT=w1w_d[:, t * P : (t + 1) * P].bitcast(FP8X4),
-                    lhsT_scale=first_scale[:, S + t * P : S + (t + 1) * P],
-                    rhs=xq_w[:, cols].bitcast(FP8X4),
-                    rhs_scale=first_scale[:, cols],
-                    start=True,
-                    stop=True,
-                )
-                y_banks[h, t] = y_ps
-        for h, t in EVAC_ORDER:
-            if h < Y_PARTS:
-                nc.scalar.activation(us[t][:, h * y_width : (h + 1) * y_width], y_banks[h, t][:], ACT.Copy, scale=gs_neg[:, t : t + 1])
-        for t in ST_ORDER:
+        hc_w_d = sb.tile([P, C], U32, name="hc_w_d", align_bytes=64)
+        deal_words(hc_w_d[:].rearrange("p (t m) -> p t m", t=PACK), hc_w[:])
+        ca_w_d = sb.tile([P, PACK, P], U32, name="ca_w_d", align_bytes=64)
+        deal_words(ca_w_d[:, :, : P // 2], ca_w0[:])
+        for t in (1, 0, 2, 3):
             u = us[t]
-            if t in FUSED_ST:
-                other = st[:, t + 2, HALF:]
+            if t < 2:
+                other = st[:, 3 - t, HALF:]
                 for h in range(2):
                     cols = slice(h * HALF, (h + 1) * HALF)
-                    nc.sync.dma_start(other[:, cols], u[:, cols])
                     nc.vector.tensor_tensor(
                         st[:, t, cols], u[:].indirect(entries(n1_l, h * HALF, HALF)), other[:, cols], ALU.subtract
                     )
             else:
                 other = reuse.tile([P, S], F32, name="other%d" % t, offset=4096 + 5120 * (t - 2), align_bytes=64)
                 nc.scalar.activation(other[:], u[:].indirect(n1_l[:]), ACT.Copy)
-                if STT:
-                    for h in range(2):
-                        cols = slice(h * HALF, (h + 1) * HALF)
-                        nc.vector.scalar_tensor_tensor(
-                            st[:, t, cols], y_banks[h, t][:], gs_abs[:, t : t + 1], other[:, cols], ALU.mult, ALU.add
-                        )
-                else:
-                    nc.vector.tensor_tensor(st[:, t, :S], other[:], u[:, :S], ALU.subtract)
+                nc.vector.tensor_tensor(st[:, t, :S], other[:], u[:, :S], ALU.subtract)
 
+        if CLOCK:
+            clock = sb.tile([P, 2], F32, name="clock")
+            nc.gpsimd.tensor_copy(clock[:, 0:1], st[:, 3, 0:1])
         a_win = [sb.tile([P, S], F32, name="a_win%d" % t, align_bytes=64) for t in range(PACK)]
         b_win = [sb.tile([P, S], F32, name="b_win%d" % t, align_bytes=64) for t in range(PACK)]
         a_own = sb.tile([P, PACK, S], F32, name="a_own", align_bytes=64)
@@ -187,12 +178,12 @@ def tile_picked_cdhnormbhopmx_none_po_kernel(
         for h in range(2):
             cols = slice(h * HALF, (h + 1) * HALF)
             st_n2 = reuse.tile([P, PACK, HALF], F32, name="st_n2_%d" % h, offset=(0, 9216)[h], align_bytes=64)
-            for t in range(PACK):
-                looked_up = st[:, t, :S].indirect(entries(n2_l, h * HALF, HALF))
-                if (h, t) in G2_ON_VECTOR:
-                    nc.vector.tensor_copy(st_n2[:, t, :], looked_up)
+            for on_vector, t, start, width in G2_PLAN[h]:
+                looked_up = st[:, t, :S].indirect(entries(n2_l, h * HALF + start, width))
+                if on_vector:
+                    nc.vector.tensor_copy(st_n2[:, t, start : start + width], looked_up)
                 else:
-                    nc.scalar.activation(st_n2[:, t, :], looked_up, ACT.Copy)
+                    nc.scalar.activation(st_n2[:, t, start : start + width], looked_up, ACT.Copy)
             parts = [slice(h * HALF + e * QUARTER, h * HALF + (e + 1) * QUARTER) for e in range(2)]
             z_abs = [sb.tile([P, QUARTER * PACK], BF16, name="z_abs%d" % e, align_bytes=64) for e in range(2)]
             z_bf = [
@@ -266,6 +257,8 @@ def tile_picked_cdhnormbhopmx_none_po_kernel(
                 nc.vector.tensor_tensor(
                     den[:, t, cols], b_win[t][:].indirect(entries(n4_l, h * HALF, HALF)), b_own[:, t, cols], ALU.add
                 )
+        if CLOCK:
+            nc.gpsimd.tensor_copy(clock[:, 1:2], den[:, 3, S - 1 : S])
         root = sb.tile([P, PACK, S], F32, name="root", align_bytes=64)
         recip = sb.tile([P, PACK, S], F32, name="recip", align_bytes=64)
         a_got = sb.tile([P, PACK, HALF], F32, name="a_got", align_bytes=64)

@@ -17,16 +17,18 @@ ACT = mybir.ActivationFunctionType
 
 P = 128
 PACK = 4
+QUADRANT = 32
+ROW_STEP = 8
+SCALE_ROWS = K // 32
 LIST_ROWS = 16
+LINE = 4
 SPARE = 16
 HALF = S // 2
 QUARTER = S // 4
-G2_PLAN = (((0,1,0,256),(0,2,0,256),(1,0,0,256),(0,3,0,128),(0,3,128,128)), ((0,0,0,128),(0,1,0,128),(0,2,0,128),(0,3,0,128),(0,0,128,128),(0,1,128,128),(0,2,128,128),(0,3,128,128)))
-WARM = True
-OWN0 = "S"
-DUP1 = "S"
-CLOCK = False
-OWN_BY_SCALAR = 2
+F32_BYTES = 4
+
+FUSED_ST_TILES = 2
+COPIED_B_TILES = 2
 
 
 def tile_picked_cdhnormbhopmx_none_po_kernel(
@@ -37,7 +39,7 @@ def tile_picked_cdhnormbhopmx_none_po_kernel(
     with ExitStack() as ctx:
         lists = ctx.enter_context(tc.tile_pool(name="lists", bufs=1))
         sb = ctx.enter_context(tc.tile_pool(name="sb", bufs=1))
-        reuse = ctx.enter_context(tc.tile_pool(name="reuse", bufs=1))
+        placed = ctx.enter_context(tc.tile_pool(name="placed", bufs=1))
         psum = ctx.enter_context(tc.psum_pool(name="psum", bufs=1))
 
         def load_list(name, src):
@@ -50,26 +52,31 @@ def tile_picked_cdhnormbhopmx_none_po_kernel(
 
         def deal_words(dst, src):
             nc.vector.tensor_copy(
-                dst.rearrange("p t (c i) -> p c t i", i=4),
-                src.rearrange("p (c i t) -> p c t i", i=4, t=PACK),
+                dst.rearrange("p t (c i) -> p c t i", i=LINE),
+                src.rearrange("p (c i t) -> p c t i", i=LINE, t=PACK),
             )
 
-        def deal(engine, dst, src):
-            engine.tensor_copy(
-                dst[:].rearrange("p (t m) -> p t m", t=PACK),
-                src[:].rearrange("p (m t) -> p t m", t=PACK),
+        def place_scale_rows(queue, tile):
+            for r in range(1, PACK):
+                queue.dma_start(tile[r:P:QUADRANT, :].bitcast(I32), tile[ROW_STEP * r : P : QUADRANT, :].bitcast(I32))
+
+        def product(out, words, scales, moving_words, moving_scales):
+            nc.tensor.matmul_mx(
+                out=out,
+                lhsT=words.bitcast(FP8X4),
+                lhsT_scale=scales,
+                rhs=moving_words.bitcast(FP8X4),
+                rhs_scale=moving_scales,
+                start=True,
+                stop=True,
             )
 
         xs = sb.tile([P, T], U8, name="xs", align_bytes=64)
         nc.vector.memset(xs[:].bitcast(I32), 0)
-        nc.sync.dma_start(xs[0:P:8, :].bitcast(I32), x_scales[0].bitcast(I32))
+        nc.sync.dma_start(xs[0:P:ROW_STEP, :].bitcast(I32), x_scales[0].bitcast(I32))
         w1s = sb.tile([P, H], U8, name="w1s", align_bytes=64)
         nc.gpsimd.memset(w1s[:].bitcast(I32), 0)
-        nc.sync.dma_start(w1s[0:P:8, :].bitcast(I32), w1_scales[0].bitcast(I32))
-
-        def place_scale_rows(queue, tile):
-            for r in range(1, PACK):
-                queue.dma_start(tile[r:P:32, :].bitcast(I32), tile[8 * r : P : 32, :].bitcast(I32))
+        nc.sync.dma_start(w1s[0:P:ROW_STEP, :].bitcast(I32), w1_scales[0].bitcast(I32))
 
         gs_t = sb.tile([P, PACK], F32, name="gs_t")
         nc.sync.dma_start(gs_t[:], gs.rearrange("(p t) o -> p (t o)", t=PACK))
@@ -85,26 +92,28 @@ def tile_picked_cdhnormbhopmx_none_po_kernel(
         n4_l = load_list("n4_l", n4)
         n3_l = load_list("n3_l", n3)
 
-        if WARM:
-            warm = sb.tile([P, 1], F32, name="warm")
-            nc.vector.memset(warm[:], 1.0)
-            warm_out = sb.tile([P, 1], F32, name="warm_out")
-            nc.scalar.activation(warm_out[:], warm[:], ACT.Abs_reciprocal_sqrt)
+        warm = sb.tile([P, 1], F32, name="warm")
+        nc.vector.memset(warm[:], 1.0)
+        warm_out = sb.tile([P, 1], F32, name="warm_out")
+        nc.scalar.activation(warm_out[:], warm[:], ACT.Abs_reciprocal_sqrt)
+
         gs_abs = sb.tile([P, PACK], F32, name="gs_abs")
         nc.scalar.activation(gs_abs[:], gs_t[:], ACT.Abs)
         gs_neg = sb.tile([P, PACK], F32, name="gs_neg")
         nc.scalar.activation(gs_neg[:], gs_abs[:], ACT.Copy, scale=-1.0)
-        sgn_bf = sb.tile([P, PACK], BF16, name="sgn_bf")
-        nc.scalar.activation(sgn_bf[:], gs_t[:], ACT.Sign)
+        gs_sign = sb.tile([P, PACK], BF16, name="gs_sign")
+        nc.scalar.activation(gs_sign[:], gs_t[:], ACT.Sign)
 
         picked_s = sb.tile([P, 2 * C], U8, name="picked_s", align_bytes=64)
         xq_s = picked_s[:, HALF : HALF + S]
         nc.vector.tensor_copy(xq_s, xs[:].indirect(offs_l[:]))
-        first_scale = sb.tile([P, S + H], U8, name="first_scale", align_bytes=64)
-        deal(nc.vector, first_scale[:, S:], w1s)
+        y_scale = sb.tile([P, S + H], U8, name="y_scale", align_bytes=64)
+        nc.vector.tensor_copy(
+            y_scale[:, S:].rearrange("p (t m) -> p t m", t=PACK), w1s[:].rearrange("p (m t) -> p t m", t=PACK)
+        )
         nc.vector.tensor_copy(picked_s[:, :HALF], xs[:].indirect(entries(ca_l, 0, HALF)))
-        nc.vector.tensor_copy(first_scale[:, :S].bitcast(I32), xq_s.bitcast(I32))
-        place_scale_rows(nc.scalar, first_scale)
+        nc.vector.tensor_copy(y_scale[:, :S].bitcast(I32), xq_s.bitcast(I32))
+        place_scale_rows(nc.scalar, y_scale)
         w1w_d = sb.tile([P, H], U32, name="w1w_d", align_bytes=64)
         deal_words(w1w_d[:].rearrange("p (t m) -> p t m", t=PACK), w1w[:])
         nc.vector.tensor_copy(picked_s[:, HALF:C], xs[:].indirect(entries(ca_l, HALF, HALF)))
@@ -120,55 +129,48 @@ def tile_picked_cdhnormbhopmx_none_po_kernel(
             picked_s[:].rearrange("p (c m t) -> p c t m", c=2, t=PACK),
         )
         place_scale_rows(nc.sync, cand_scale)
-        ca_w0 = sb.tile([P, HALF], U32, name="ca_w0", align_bytes=64)
-        nc.vector.tensor_copy(ca_w0[:], xw[:].indirect(entries(ca_l, 0, HALF)))
+        ca_w_early = sb.tile([P, HALF], U32, name="ca_w_early", align_bytes=64)
+        nc.vector.tensor_copy(ca_w_early[:], xw[:].indirect(entries(ca_l, 0, HALF)))
 
         st = sb.tile([P, PACK, S + HALF], F32, name="st", align_bytes=64)
-        us = []
+        u_copy = [st[:, PACK - 1 - t, HALF:] for t in range(FUSED_ST_TILES)]
+        u = []
         for t in range(PACK):
             y_ps = psum.tile([P, S], F32, name="y_ps", tag="bank%d" % t)
-            nc.tensor.matmul_mx(
-                out=y_ps[:],
-                lhsT=w1w_d[:, t * P : (t + 1) * P].bitcast(FP8X4),
-                lhsT_scale=first_scale[:, S + t * P : S + (t + 1) * P],
-                rhs=xq_w[:].bitcast(FP8X4),
-                rhs_scale=first_scale[:, :S],
-                start=True,
-                stop=True,
+            product(
+                y_ps[:], w1w_d[:, t * P : (t + 1) * P], y_scale[:, S + t * P : S + (t + 1) * P], xq_w[:], y_scale[:, :S]
             )
-            spare = 0 if t < 2 else SPARE
-            u = sb.tile([P, S + spare], F32, name="u%d" % t, align_bytes=64)
+            spare = 0 if t < FUSED_ST_TILES else SPARE
+            u_t = sb.tile([P, S + spare], F32, name="u%d" % t, align_bytes=64)
             if spare:
-                nc.vector.memset(u[:, S:], 0.0)
-            nc.scalar.activation(u[:, :S], y_ps[:], ACT.Copy, scale=gs_neg[:, t : t + 1])
+                nc.vector.memset(u_t[:, S:], 0.0)
+            nc.scalar.activation(u_t[:, :S], y_ps[:], ACT.Copy, scale=gs_neg[:, t : t + 1])
             if t == 0:
-                (nc.scalar if DUP1 == "S" else nc.sync).dma_start(st[:, 3, HALF:], u[:])
-            if t == 1 and OWN0 == "V":
-                nc.vector.tensor_scalar(st[:, 2, HALF:], y_ps[:], gs_neg[:, t : t + 1], None, ALU.mult)
-            if t == 1 and OWN0 == "S":
-                nc.scalar.activation(st[:, 2, HALF:], y_ps[:], ACT.Copy, scale=gs_neg[:, t : t + 1])
-            us.append(u)
+                nc.scalar.dma_start(u_copy[t], u_t[:])
+            elif t < FUSED_ST_TILES:
+                nc.scalar.activation(u_copy[t], y_ps[:], ACT.Copy, scale=gs_neg[:, t : t + 1])
+            u.append(u_t)
         hc_w_d = sb.tile([P, C], U32, name="hc_w_d", align_bytes=64)
         deal_words(hc_w_d[:].rearrange("p (t m) -> p t m", t=PACK), hc_w[:])
         ca_w_d = sb.tile([P, PACK, P], U32, name="ca_w_d", align_bytes=64)
-        deal_words(ca_w_d[:, :, : P // 2], ca_w0[:])
-        for t in (1, 0, 2, 3):
-            u = us[t]
-            if t < 2:
-                other = st[:, 3 - t, HALF:]
-                for h in range(2):
-                    cols = slice(h * HALF, (h + 1) * HALF)
-                    nc.vector.tensor_tensor(
-                        st[:, t, cols], u[:].indirect(entries(n1_l, h * HALF, HALF)), other[:, cols], ALU.subtract
-                    )
-            else:
-                other = reuse.tile([P, S], F32, name="other%d" % t, offset=4096 + 5120 * (t - 2), align_bytes=64)
-                nc.scalar.activation(other[:], u[:].indirect(n1_l[:]), ACT.Copy)
-                nc.vector.tensor_tensor(st[:, t, :S], other[:], u[:, :S], ALU.subtract)
+        deal_words(ca_w_d[:, :, : P // 2], ca_w_early[:])
 
-        if CLOCK:
-            clock = sb.tile([P, 2], F32, name="clock")
-            nc.gpsimd.tensor_copy(clock[:, 0:1], st[:, 3, 0:1])
+        half_bytes = PACK * HALF * F32_BYTES
+        last_at = half_bytes + S * F32_BYTES
+        u_n1_at = {PACK - 2: half_bytes, PACK - 1: last_at}
+        st_n2_at = (0, last_at)
+
+        for t in reversed(range(FUSED_ST_TILES)):
+            for start in (0, HALF):
+                cols = slice(start, start + HALF)
+                nc.vector.tensor_tensor(
+                    st[:, t, cols], u[t][:].indirect(entries(n1_l, start, HALF)), u_copy[t][:, cols], ALU.subtract
+                )
+        for t in range(FUSED_ST_TILES, PACK):
+            u_n1 = placed.tile([P, S], F32, name="u_n1_%d" % t, offset=u_n1_at[t], align_bytes=64)
+            nc.scalar.activation(u_n1[:], u[t][:].indirect(n1_l[:]), ACT.Copy)
+            nc.vector.tensor_tensor(st[:, t, :S], u_n1[:], u[t][:, :S], ALU.subtract)
+
         a_win = [sb.tile([P, S], F32, name="a_win%d" % t, align_bytes=64) for t in range(PACK)]
         b_win = [sb.tile([P, S], F32, name="b_win%d" % t, align_bytes=64) for t in range(PACK)]
         a_own = sb.tile([P, PACK, S], F32, name="a_own", align_bytes=64)
@@ -177,146 +179,154 @@ def tile_picked_cdhnormbhopmx_none_po_kernel(
         z_s = sb.tile([P, S], U8, name="z_s", align_bytes=64)
         for h in range(2):
             cols = slice(h * HALF, (h + 1) * HALF)
-            st_n2 = reuse.tile([P, PACK, HALF], F32, name="st_n2_%d" % h, offset=(0, 9216)[h], align_bytes=64)
-            for on_vector, t, start, width in G2_PLAN[h]:
-                looked_up = st[:, t, :S].indirect(entries(n2_l, h * HALF + start, width))
-                if on_vector:
-                    nc.vector.tensor_copy(st_n2[:, t, start : start + width], looked_up)
-                else:
-                    nc.scalar.activation(st_n2[:, t, start : start + width], looked_up, ACT.Copy)
+            st_n2 = placed.tile([P, PACK, HALF], F32, name="st_n2_%d" % h, offset=st_n2_at[h], align_bytes=64)
+
+            def st_looked_up(t, start, width):
+                return st[:, t, :S].indirect(entries(n2_l, h * HALF + start, width))
+
+            if h == 0:
+                for t in range(1, PACK - 1):
+                    nc.scalar.activation(st_n2[:, t, :], st_looked_up(t, 0, HALF), ACT.Copy)
+                nc.vector.tensor_copy(st_n2[:, 0, :], st_looked_up(0, 0, HALF))
+                quartered = [PACK - 1]
+            else:
+                quartered = range(PACK)
+            for start in (0, QUARTER):
+                for t in quartered:
+                    nc.scalar.activation(
+                        st_n2[:, t, start : start + QUARTER], st_looked_up(t, start, QUARTER), ACT.Copy
+                    )
+
             parts = [slice(h * HALF + e * QUARTER, h * HALF + (e + 1) * QUARTER) for e in range(2)]
-            z_abs = [sb.tile([P, QUARTER * PACK], BF16, name="z_abs%d" % e, align_bytes=64) for e in range(2)]
+            z_unsigned = [
+                sb.tile([P, QUARTER * PACK], BF16, name="z_unsigned%d" % e, align_bytes=64) for e in range(2)
+            ]
             z_bf = [
-                sb.tile([P, QUARTER * PACK], BF16, name="z_bf", tag="slot_z%d%d" % (h, e), align_bytes=64)
+                sb.tile([P, QUARTER * PACK], BF16, name="z_bf", tag="z_bf%d%d" % (h, e), align_bytes=64)
                 for e in range(2)
             ]
             for e, part in enumerate(parts):
                 nc.vector.tensor_tensor(
-                    z_abs[e][:].rearrange("p (c i t) -> p c t i", i=4, t=PACK),
-                    st[:, :, part].rearrange("p t (c i) -> p c t i", i=4),
-                    st_n2[:, :, e * QUARTER : (e + 1) * QUARTER].rearrange("p t (c i) -> p c t i", i=4),
+                    z_unsigned[e][:].rearrange("p (c i t) -> p c t i", i=LINE, t=PACK),
+                    st[:, :, part].rearrange("p t (c i) -> p c t i", i=LINE),
+                    st_n2[:, :, e * QUARTER : (e + 1) * QUARTER].rearrange("p t (c i) -> p c t i", i=LINE),
                     ALU.max,
                 )
             for e in range(2):
                 nc.vector.tensor_tensor(
                     z_bf[e][:].rearrange("p (j t) -> p j t", t=PACK),
-                    z_abs[e][:].rearrange("p (j t) -> p j t", t=PACK),
-                    sgn_bf[:].unsqueeze(1).to_broadcast([P, QUARTER, PACK]),
+                    z_unsigned[e][:].rearrange("p (j t) -> p j t", t=PACK),
+                    gs_sign[:].unsqueeze(1).to_broadcast([P, QUARTER, PACK]),
                     ALU.mult,
                 )
             for e, part in enumerate(parts):
                 nc.vector.quantize_mx(out=z_w[:, part].bitcast(FP8X4), scales=z_s[:, part], in_=z_bf[e][:])
-            twice = []
+            b_banks = []
             for t in range(PACK):
-                rows = slice(t * P, (t + 1) * P)
                 b_ps = psum.tile([P, HALF], F32, name="b_ps", tag="bank%d" % (PACK + (t + 2 * h) % PACK))
-                nc.tensor.matmul_mx(
-                    out=b_ps[:],
-                    lhsT=hc_w_d[:, rows].bitcast(FP8X4),
-                    lhsT_scale=cand_scale[:, C + t * P : C + (t + 1) * P],
-                    rhs=z_w[:, cols].bitcast(FP8X4),
-                    rhs_scale=z_s[:, cols],
-                    start=True,
-                    stop=True,
+                product(
+                    b_ps[:],
+                    hc_w_d[:, t * P : (t + 1) * P],
+                    cand_scale[:, C + t * P : C + (t + 1) * P],
+                    z_w[:, cols],
+                    z_s[:, cols],
                 )
                 nc.scalar.activation(b_win[t][:, cols], b_ps[:], ACT.Abs)
-                if h == 0 and t < OWN_BY_SCALAR:
-                    twice.append((t, b_ps))
+                if h == 0 and t < COPIED_B_TILES:
+                    b_banks.append(b_ps)
                 else:
                     nc.sync.dma_start(b_own[:, t, cols], b_win[t][:, cols])
-            for t, b_ps in twice:
+            for t, b_ps in enumerate(b_banks):
                 nc.scalar.activation(b_own[:, t, cols], b_ps[:], ACT.Abs)
 
-        ca_w1 = sb.tile([P, HALF], U32, name="ca_w1", tag="slot_z10", align_bytes=64)
-        nc.vector.tensor_copy(ca_w1[:], xw[:].indirect(entries(ca_l, HALF, HALF)))
-        deal_words(ca_w_d[:, :, P // 2 :], ca_w1[:])
+        ca_w_late = sb.tile([P, HALF], U32, name="ca_w_late", tag="z_bf10", align_bytes=64)
+        nc.vector.tensor_copy(ca_w_late[:], xw[:].indirect(entries(ca_l, HALF, HALF)))
+        deal_words(ca_w_d[:, :, P // 2 :], ca_w_late[:])
         for t in range(PACK):
-            rows = slice(t * P, (t + 1) * P)
             a_ps = psum.tile([P, S], F32, name="a_ps", tag="bank%d" % t)
-            nc.tensor.matmul_mx(
-                out=a_ps[:],
-                lhsT=ca_w_d[:, t, :].bitcast(FP8X4),
-                lhsT_scale=cand_scale[:, rows],
-                rhs=z_w[:].bitcast(FP8X4),
-                rhs_scale=z_s[:],
-                start=True,
-                stop=True,
-            )
+            product(a_ps[:], ca_w_d[:, t, :], cand_scale[:, t * P : (t + 1) * P], z_w[:], z_s[:])
             nc.scalar.activation(a_win[t][:], a_ps[:], ACT.Copy, scale=-1.0)
             nc.sync.dma_start(a_own[:, t, :], a_win[t][:])
 
         out_rows = out_0.rearrange("(p t) j -> p t j", t=PACK)
         words_out = out_1[0].rearrange("p n t -> p (n t)").bitcast(I32)
         o_s = sb.tile([P, S], U8, name="o_s", align_bytes=64)
-        first, second = slice(0, HALF), slice(HALF, S)
-        quarters = [slice(HALF + e * QUARTER, HALF + (e + 1) * QUARTER) for e in range(2)]
+        first = slice(0, HALF)
+        late_quarters = [slice(HALF + e * QUARTER, HALF + (e + 1) * QUARTER) for e in range(2)]
 
         den = sb.tile([P, PACK, S], F32, name="den", align_bytes=64)
-        for h, cols in enumerate((first, second)):
+        for start in (0, HALF):
+            cols = slice(start, start + HALF)
             for t in range(PACK):
                 nc.vector.tensor_tensor(
-                    den[:, t, cols], b_win[t][:].indirect(entries(n4_l, h * HALF, HALF)), b_own[:, t, cols], ALU.add
+                    den[:, t, cols], b_win[t][:].indirect(entries(n4_l, start, HALF)), b_own[:, t, cols], ALU.add
                 )
-        if CLOCK:
-            nc.gpsimd.tensor_copy(clock[:, 1:2], den[:, 3, S - 1 : S])
         root = sb.tile([P, PACK, S], F32, name="root", align_bytes=64)
         recip = sb.tile([P, PACK, S], F32, name="recip", align_bytes=64)
-        a_got = sb.tile([P, PACK, HALF], F32, name="a_got", align_bytes=64)
+        a_n3 = sb.tile([P, PACK, HALF], F32, name="a_n3", align_bytes=64)
 
-        def fetch(t):
-            nc.scalar.activation(a_got[:, t, :], a_win[t][:].indirect(entries(n3_l, HALF, HALF)), ACT.Copy)
+        def fetch_late(t):
+            nc.scalar.activation(a_n3[:, t, :], a_win[t][:].indirect(entries(n3_l, HALF, HALF)), ACT.Copy)
 
         nc.scalar.activation(root[:, :, first], den[:, :, first], ACT.Abs_reciprocal_sqrt, bias=8.0)
-        fetch(0)
+        fetch_late(0)
         nc.scalar.activation(recip[:, :, first], root[:, :, first], ACT.Square)
         for t in range(1, PACK):
-            fetch(t)
-        for cols in quarters:
+            fetch_late(t)
+        for cols in late_quarters:
             nc.scalar.activation(root[:, :, cols], den[:, :, cols], ACT.Abs_reciprocal_sqrt, bias=8.0)
-        for cols in quarters:
+        for cols in late_quarters:
             nc.scalar.activation(recip[:, :, cols], root[:, :, cols], ACT.Square)
 
         res = sb.tile([P, PACK, S], F32, name="res", align_bytes=64)
         num = sb.tile([P, PACK, HALF], F32, name="num", align_bytes=64)
-        for t in range(PACK):
-            width = QUARTER if t == PACK - 1 else HALF
-            for start in range(0, HALF, width):
-                cols = slice(start, start + width)
-                nc.vector.tensor_tensor(
-                    num[:, t, cols], a_win[t][:].indirect(entries(n3_l, start, width)), a_own[:, t, cols], ALU.subtract
-                )
-        for e in range(2):
-            cols = slice(e * QUARTER, (e + 1) * QUARTER)
+
+        def fused_numerator(t, start, width):
+            nc.vector.tensor_tensor(
+                num[:, t, start : start + width],
+                a_win[t][:].indirect(entries(n3_l, start, width)),
+                a_own[:, t, start : start + width],
+                ALU.subtract,
+            )
+
+        for t in range(PACK - 1):
+            fused_numerator(t, 0, HALF)
+        for start in (0, QUARTER):
+            fused_numerator(PACK - 1, start, QUARTER)
+        for start in (0, QUARTER):
+            cols = slice(start, start + QUARTER)
             nc.vector.tensor_tensor(res[:, :, cols], num[:, :, cols], recip[:, :, cols], ALU.mult)
         nc.sync.dma_start(out_rows[:, :, first], res[:, :, first])
 
-        def round_and_pack(copy, cols, name):
-            width = cols.stop - cols.start
-            res_bf = sb.tile([P, width * PACK], BF16, name=name, align_bytes=64)
+        def round_and_interleave(copy, cols, name):
+            res_bf = sb.tile([P, (cols.stop - cols.start) * PACK], BF16, name=name, align_bytes=64)
             copy(
-                res_bf[:].rearrange("p (c i t) -> p c t i", i=4, t=PACK),
-                res[:, :, cols].rearrange("p t (c i) -> p c t i", i=4),
+                res_bf[:].rearrange("p (c i t) -> p c t i", i=LINE, t=PACK),
+                res[:, :, cols].rearrange("p t (c i) -> p c t i", i=LINE),
             )
             return res_bf
 
         o_w = sb.tile([P, S], U32, name="o_w", align_bytes=64)
 
-        def quantise(cols, res_bf):
+        def quantise_result(cols, res_bf):
             nc.vector.quantize_mx(out=o_w[:, cols].bitcast(FP8X4), scales=o_s[:, cols], in_=res_bf[:])
 
-        first_bf = round_and_pack(nc.scalar.copy, first, "first_bf")
-        for e, cols in enumerate(quarters):
+        first_bf = round_and_interleave(nc.scalar.copy, first, "first_bf")
+        for e, cols in enumerate(late_quarters):
             part = slice(e * QUARTER, (e + 1) * QUARTER)
-            nc.vector.tensor_tensor(num[:, :, part], a_got[:, :, part], a_own[:, :, cols], ALU.subtract)
-        for e, cols in enumerate(quarters):
-            nc.vector.tensor_tensor(res[:, :, cols], num[:, :, e * QUARTER : (e + 1) * QUARTER], recip[:, :, cols], ALU.mult)
+            nc.vector.tensor_tensor(num[:, :, part], a_n3[:, :, part], a_own[:, :, cols], ALU.subtract)
+        for e, cols in enumerate(late_quarters):
+            part = slice(e * QUARTER, (e + 1) * QUARTER)
+            nc.vector.tensor_tensor(res[:, :, cols], num[:, :, part], recip[:, :, cols], ALU.mult)
             nc.sync.dma_start(out_rows[:, :, cols], res[:, :, cols])
-        late_bf = [round_and_pack(nc.vector.tensor_copy, cols, "late_bf%d" % e) for e, cols in enumerate(quarters)]
-        quantise(quarters[0], late_bf[0])
-        quantise(first, first_bf)
-        quantise(quarters[1], late_bf[1])
+        late_bf = [
+            round_and_interleave(nc.vector.tensor_copy, cols, "late_bf%d" % e) for e, cols in enumerate(late_quarters)
+        ]
+        quantise_result(late_quarters[0], late_bf[0])
+        quantise_result(first, first_bf)
+        quantise_result(late_quarters[1], late_bf[1])
         nc.scalar.dma_start(words_out[:, : S - QUARTER], o_w[:, : S - QUARTER].bitcast(I32))
         nc.sync.dma_start(words_out[:, S - QUARTER :], o_w[:, S - QUARTER :].bitcast(I32))
         for r in range(PACK):
             queue = nc.sync if r % 2 == 0 else nc.scalar
-            queue.dma_start(out_2[0, r:16:PACK, :].bitcast(I32), o_s[r:P:32, :].bitcast(I32))
+            queue.dma_start(out_2[0, r:SCALE_ROWS:PACK, :].bitcast(I32), o_s[r:P:QUADRANT, :].bitcast(I32))

from contextlib import ExitStack

import concourse.mybir as mybir

K, T, S, H, C = 512, 2048, 512, 512, 512
FLOPS = 2 * K * H * S + 2 * 2 * K * C * S

F32 = mybir.dt.float32
BF16 = mybir.dt.bfloat16
I32 = mybir.dt.int32
U32 = mybir.dt.uint32
U16 = mybir.dt.uint16
U8 = mybir.dt.uint8
FP8X4 = mybir.dt.float8_e4m3fn_x4
ALU = mybir.AluOpType
ACT = mybir.ActivationFunctionType

P = 128
PACK = 4
QUADRANT = 32
ROW_STEP = 8
SCALE_ROWS = K // 32
LIST_ROWS = 16
LINE = 4
SPARE = 16
HALF = S // 2
QUARTER = S // 4
F32_BYTES = 4

FUSED_ST_TILES = 2
COPIED_B_TILES = 2


def tile_picked_cdhnormbhopmx_none_po_kernel(
    tc, x_words, x_scales, w1_words, w1_scales, gs, offs, n1, n2, ca, hc, n3, n4, out_0, out_1, out_2
):
    nc = tc.nc

    with ExitStack() as ctx:
        lists = ctx.enter_context(tc.tile_pool(name="lists", bufs=1))
        sb = ctx.enter_context(tc.tile_pool(name="sb", bufs=1))
        placed = ctx.enter_context(tc.tile_pool(name="placed", bufs=1))
        psum = ctx.enter_context(tc.psum_pool(name="psum", bufs=1))

        def load_list(name, src):
            tile = lists.tile([P, S // LIST_ROWS], U16, name=name)
            nc.sync.dma_start(tile[:], src)
            return tile

        def entries(list_tile, start, count):
            return list_tile[:, start // LIST_ROWS : (start + count) // LIST_ROWS]

        def deal_words(dst, src):
            nc.vector.tensor_copy(
                dst.rearrange("p t (c i) -> p c t i", i=LINE),
                src.rearrange("p (c i t) -> p c t i", i=LINE, t=PACK),
            )

        def place_scale_rows(queue, tile):
            for r in range(1, PACK):
                queue.dma_start(tile[r:P:QUADRANT, :].bitcast(I32), tile[ROW_STEP * r : P : QUADRANT, :].bitcast(I32))

        def product(out, words, scales, moving_words, moving_scales):
            nc.tensor.matmul_mx(
                out=out,
                lhsT=words.bitcast(FP8X4),
                lhsT_scale=scales,
                rhs=moving_words.bitcast(FP8X4),
                rhs_scale=moving_scales,
                start=True,
                stop=True,
            )

        xs = sb.tile([P, T], U8, name="xs", align_bytes=64)
        nc.vector.memset(xs[:].bitcast(I32), 0)
        nc.sync.dma_start(xs[0:P:ROW_STEP, :].bitcast(I32), x_scales[0].bitcast(I32))
        w1s = sb.tile([P, H], U8, name="w1s", align_bytes=64)
        nc.gpsimd.memset(w1s[:].bitcast(I32), 0)
        nc.sync.dma_start(w1s[0:P:ROW_STEP, :].bitcast(I32), w1_scales[0].bitcast(I32))

        gs_t = sb.tile([P, PACK], F32, name="gs_t")
        nc.sync.dma_start(gs_t[:], gs.rearrange("(p t) o -> p (t o)", t=PACK))
        offs_l = load_list("offs_l", offs)
        ca_l = load_list("ca_l", ca)
        n1_l = load_list("n1_l", n1)
        w1w = sb.tile([P, H], U32, name="w1w", align_bytes=64)
        nc.sync.dma_start(w1w[:].bitcast(I32), w1_words[0].rearrange("p n t -> p (n t)").bitcast(I32))
        xw = sb.tile([P, T], U32, name="xw", align_bytes=64)
        nc.sync.dma_start(xw[:].bitcast(I32), x_words[0].rearrange("p n t -> p (n t)").bitcast(I32))
        hc_l = load_list("hc_l", hc)
        n2_l = load_list("n2_l", n2)
        n4_l = load_list("n4_l", n4)
        n3_l = load_list("n3_l", n3)

        warm = sb.tile([P, 1], F32, name="warm")
        nc.vector.memset(warm[:], 1.0)
        warm_out = sb.tile([P, 1], F32, name="warm_out")
        nc.scalar.activation(warm_out[:], warm[:], ACT.Abs_reciprocal_sqrt)

        gs_abs = sb.tile([P, PACK], F32, name="gs_abs")
        nc.scalar.activation(gs_abs[:], gs_t[:], ACT.Abs)
        gs_neg = sb.tile([P, PACK], F32, name="gs_neg")
        nc.scalar.activation(gs_neg[:], gs_abs[:], ACT.Copy, scale=-1.0)
        gs_sign = sb.tile([P, PACK], BF16, name="gs_sign")
        nc.scalar.activation(gs_sign[:], gs_t[:], ACT.Sign)

        picked_s = sb.tile([P, 2 * C], U8, name="picked_s", align_bytes=64)
        xq_s = picked_s[:, HALF : HALF + S]
        nc.vector.tensor_copy(xq_s, xs[:].indirect(offs_l[:]))
        y_scale = sb.tile([P, S + H], U8, name="y_scale", align_bytes=64)
        nc.vector.tensor_copy(
            y_scale[:, S:].rearrange("p (t m) -> p t m", t=PACK), w1s[:].rearrange("p (m t) -> p t m", t=PACK)
        )
        nc.vector.tensor_copy(picked_s[:, :HALF], xs[:].indirect(entries(ca_l, 0, HALF)))
        nc.vector.tensor_copy(y_scale[:, :S].bitcast(I32), xq_s.bitcast(I32))
        place_scale_rows(nc.scalar, y_scale)
        w1w_d = sb.tile([P, H], U32, name="w1w_d", align_bytes=64)
        deal_words(w1w_d[:].rearrange("p (t m) -> p t m", t=PACK), w1w[:])
        nc.vector.tensor_copy(picked_s[:, HALF:C], xs[:].indirect(entries(ca_l, HALF, HALF)))
        xq_w = sb.tile([P, S], U32, name="xq_w", align_bytes=64)
        nc.vector.tensor_copy(xq_w[:], xw[:].indirect(offs_l[:]))

        nc.vector.tensor_copy(picked_s[:, C:], xs[:].indirect(hc_l[:]))
        hc_w = sb.tile([P, C], U32, name="hc_w", align_bytes=64)
        nc.vector.tensor_copy(hc_w[:], xw[:].indirect(hc_l[:]))
        cand_scale = sb.tile([P, 2 * C], U8, name="cand_scale", align_bytes=64)
        nc.vector.tensor_copy(
            cand_scale[:].rearrange("p (c t m) -> p c t m", c=2, t=PACK),
            picked_s[:].rearrange("p (c m t) -> p c t m", c=2, t=PACK),
        )
        place_scale_rows(nc.sync, cand_scale)
        ca_w_early = sb.tile([P, HALF], U32, name="ca_w_early", align_bytes=64)
        nc.vector.tensor_copy(ca_w_early[:], xw[:].indirect(entries(ca_l, 0, HALF)))

        st = sb.tile([P, PACK, S + HALF], F32, name="st", align_bytes=64)
        u_copy = [st[:, PACK - 1 - t, HALF:] for t in range(FUSED_ST_TILES)]
        u = []
        for t in range(PACK):
            y_ps = psum.tile([P, S], F32, name="y_ps", tag="bank%d" % t)
            product(
                y_ps[:], w1w_d[:, t * P : (t + 1) * P], y_scale[:, S + t * P : S + (t + 1) * P], xq_w[:], y_scale[:, :S]
            )
            spare = 0 if t < FUSED_ST_TILES else SPARE
            u_t = sb.tile([P, S + spare], F32, name="u%d" % t, align_bytes=64)
            if spare:
                nc.vector.memset(u_t[:, S:], 0.0)
            nc.scalar.activation(u_t[:, :S], y_ps[:], ACT.Copy, scale=gs_neg[:, t : t + 1])
            if t == 0:
                nc.scalar.dma_start(u_copy[t], u_t[:])
            elif t < FUSED_ST_TILES:
                nc.scalar.activation(u_copy[t], y_ps[:], ACT.Copy, scale=gs_neg[:, t : t + 1])
            u.append(u_t)
        hc_w_d = sb.tile([P, C], U32, name="hc_w_d", align_bytes=64)
        deal_words(hc_w_d[:].rearrange("p (t m) -> p t m", t=PACK), hc_w[:])
        ca_w_d = sb.tile([P, PACK, P], U32, name="ca_w_d", align_bytes=64)
        deal_words(ca_w_d[:, :, : P // 2], ca_w_early[:])

        half_bytes = PACK * HALF * F32_BYTES
        last_at = half_bytes + S * F32_BYTES
        u_n1_at = {PACK - 2: half_bytes, PACK - 1: last_at}
        st_n2_at = (0, last_at)

        for t in reversed(range(FUSED_ST_TILES)):
            for start in (0, HALF):
                cols = slice(start, start + HALF)
                nc.vector.tensor_tensor(
                    st[:, t, cols], u[t][:].indirect(entries(n1_l, start, HALF)), u_copy[t][:, cols], ALU.subtract
                )
        for t in range(FUSED_ST_TILES, PACK):
            u_n1 = placed.tile([P, S], F32, name="u_n1_%d" % t, offset=u_n1_at[t], align_bytes=64)
            nc.scalar.activation(u_n1[:], u[t][:].indirect(n1_l[:]), ACT.Copy)
            nc.vector.tensor_tensor(st[:, t, :S], u_n1[:], u[t][:, :S], ALU.subtract)

        a_win = [sb.tile([P, S], F32, name="a_win%d" % t, align_bytes=64) for t in range(PACK)]
        b_win = [sb.tile([P, S], F32, name="b_win%d" % t, align_bytes=64) for t in range(PACK)]
        a_own = sb.tile([P, PACK, S], F32, name="a_own", align_bytes=64)
        b_own = sb.tile([P, PACK, S], F32, name="b_own", align_bytes=64)
        z_w = sb.tile([P, S], U32, name="z_w", align_bytes=64)
        z_s = sb.tile([P, S], U8, name="z_s", align_bytes=64)
        for h in range(2):
            cols = slice(h * HALF, (h + 1) * HALF)
            st_n2 = placed.tile([P, PACK, HALF], F32, name="st_n2_%d" % h, offset=st_n2_at[h], align_bytes=64)

            def st_looked_up(t, start, width):
                return st[:, t, :S].indirect(entries(n2_l, h * HALF + start, width))

            if h == 0:
                for t in range(1, PACK - 1):
                    nc.scalar.activation(st_n2[:, t, :], st_looked_up(t, 0, HALF), ACT.Copy)
                nc.vector.tensor_copy(st_n2[:, 0, :], st_looked_up(0, 0, HALF))
                quartered = [PACK - 1]
            else:
                quartered = range(PACK)
            for start in (0, QUARTER):
                for t in quartered:
                    nc.scalar.activation(
                        st_n2[:, t, start : start + QUARTER], st_looked_up(t, start, QUARTER), ACT.Copy
                    )

            parts = [slice(h * HALF + e * QUARTER, h * HALF + (e + 1) * QUARTER) for e in range(2)]
            z_unsigned = [
                sb.tile([P, QUARTER * PACK], BF16, name="z_unsigned%d" % e, align_bytes=64) for e in range(2)
            ]
            z_bf = [
                sb.tile([P, QUARTER * PACK], BF16, name="z_bf", tag="z_bf%d%d" % (h, e), align_bytes=64)
                for e in range(2)
            ]
            for e, part in enumerate(parts):
                nc.vector.tensor_tensor(
                    z_unsigned[e][:].rearrange("p (c i t) -> p c t i", i=LINE, t=PACK),
                    st[:, :, part].rearrange("p t (c i) -> p c t i", i=LINE),
                    st_n2[:, :, e * QUARTER : (e + 1) * QUARTER].rearrange("p t (c i) -> p c t i", i=LINE),
                    ALU.max,
                )
            for e in range(2):
                nc.vector.tensor_tensor(
                    z_bf[e][:].rearrange("p (j t) -> p j t", t=PACK),
                    z_unsigned[e][:].rearrange("p (j t) -> p j t", t=PACK),
                    gs_sign[:].unsqueeze(1).to_broadcast([P, QUARTER, PACK]),
                    ALU.mult,
                )
            for e, part in enumerate(parts):
                nc.vector.quantize_mx(out=z_w[:, part].bitcast(FP8X4), scales=z_s[:, part], in_=z_bf[e][:])
            b_banks = []
            for t in range(PACK):
                b_ps = psum.tile([P, HALF], F32, name="b_ps", tag="bank%d" % (PACK + (t + 2 * h) % PACK))
                product(
                    b_ps[:],
                    hc_w_d[:, t * P : (t + 1) * P],
                    cand_scale[:, C + t * P : C + (t + 1) * P],
                    z_w[:, cols],
                    z_s[:, cols],
                )
                nc.scalar.activation(b_win[t][:, cols], b_ps[:], ACT.Abs)
                if h == 0 and t < COPIED_B_TILES:
                    b_banks.append(b_ps)
                else:
                    nc.sync.dma_start(b_own[:, t, cols], b_win[t][:, cols])
            for t, b_ps in enumerate(b_banks):
                nc.scalar.activation(b_own[:, t, cols], b_ps[:], ACT.Abs)

        ca_w_late = sb.tile([P, HALF], U32, name="ca_w_late", tag="z_bf10", align_bytes=64)
        nc.vector.tensor_copy(ca_w_late[:], xw[:].indirect(entries(ca_l, HALF, HALF)))
        deal_words(ca_w_d[:, :, P // 2 :], ca_w_late[:])
        for t in range(PACK):
            a_ps = psum.tile([P, S], F32, name="a_ps", tag="bank%d" % t)
            product(a_ps[:], ca_w_d[:, t, :], cand_scale[:, t * P : (t + 1) * P], z_w[:], z_s[:])
            nc.scalar.activation(a_win[t][:], a_ps[:], ACT.Copy, scale=-1.0)
            nc.sync.dma_start(a_own[:, t, :], a_win[t][:])

        out_rows = out_0.rearrange("(p t) j -> p t j", t=PACK)
        words_out = out_1[0].rearrange("p n t -> p (n t)").bitcast(I32)
        o_s = sb.tile([P, S], U8, name="o_s", align_bytes=64)
        first = slice(0, HALF)
        late_quarters = [slice(HALF + e * QUARTER, HALF + (e + 1) * QUARTER) for e in range(2)]

        den = sb.tile([P, PACK, S], F32, name="den", align_bytes=64)
        for start in (0, HALF):
            cols = slice(start, start + HALF)
            for t in range(PACK):
                nc.vector.tensor_tensor(
                    den[:, t, cols], b_win[t][:].indirect(entries(n4_l, start, HALF)), b_own[:, t, cols], ALU.add
                )
        root = sb.tile([P, PACK, S], F32, name="root", align_bytes=64)
        recip = sb.tile([P, PACK, S], F32, name="recip", align_bytes=64)
        a_n3 = sb.tile([P, PACK, HALF], F32, name="a_n3", align_bytes=64)

        def fetch_late(t):
            nc.scalar.activation(a_n3[:, t, :], a_win[t][:].indirect(entries(n3_l, HALF, HALF)), ACT.Copy)

        nc.scalar.activation(root[:, :, first], den[:, :, first], ACT.Abs_reciprocal_sqrt, bias=8.0)
        fetch_late(0)
        nc.scalar.activation(recip[:, :, first], root[:, :, first], ACT.Square)
        for t in range(1, PACK):
            fetch_late(t)
        for cols in late_quarters:
            nc.scalar.activation(root[:, :, cols], den[:, :, cols], ACT.Abs_reciprocal_sqrt, bias=8.0)
        for cols in late_quarters:
            nc.scalar.activation(recip[:, :, cols], root[:, :, cols], ACT.Square)

        res = sb.tile([P, PACK, S], F32, name="res", align_bytes=64)
        num = sb.tile([P, PACK, HALF], F32, name="num", align_bytes=64)

        def fused_numerator(t, start, width):
            nc.vector.tensor_tensor(
                num[:, t, start : start + width],
                a_win[t][:].indirect(entries(n3_l, start, width)),
                a_own[:, t, start : start + width],
                ALU.subtract,
            )

        for t in range(PACK - 1):
            fused_numerator(t, 0, HALF)
        for start in (0, QUARTER):
            fused_numerator(PACK - 1, start, QUARTER)
        for start in (0, QUARTER):
            cols = slice(start, start + QUARTER)
            nc.vector.tensor_tensor(res[:, :, cols], num[:, :, cols], recip[:, :, cols], ALU.mult)
        nc.sync.dma_start(out_rows[:, :, first], res[:, :, first])

        def round_and_interleave(copy, cols, name):
            res_bf = sb.tile([P, (cols.stop - cols.start) * PACK], BF16, name=name, align_bytes=64)
            copy(
                res_bf[:].rearrange("p (c i t) -> p c t i", i=LINE, t=PACK),
                res[:, :, cols].rearrange("p t (c i) -> p c t i", i=LINE),
            )
            return res_bf

        o_w = sb.tile([P, S], U32, name="o_w", align_bytes=64)

        def quantise_result(cols, res_bf):
            nc.vector.quantize_mx(out=o_w[:, cols].bitcast(FP8X4), scales=o_s[:, cols], in_=res_bf[:])

        first_bf = round_and_interleave(nc.scalar.copy, first, "first_bf")
        for e, cols in enumerate(late_quarters):
            part = slice(e * QUARTER, (e + 1) * QUARTER)
            nc.vector.tensor_tensor(num[:, :, part], a_n3[:, :, part], a_own[:, :, cols], ALU.subtract)
        for e, cols in enumerate(late_quarters):
            part = slice(e * QUARTER, (e + 1) * QUARTER)
            nc.vector.tensor_tensor(res[:, :, cols], num[:, :, part], recip[:, :, cols], ALU.mult)
            nc.sync.dma_start(out_rows[:, :, cols], res[:, :, cols])
        late_bf = [
            round_and_interleave(nc.vector.tensor_copy, cols, "late_bf%d" % e) for e, cols in enumerate(late_quarters)
        ]
        quantise_result(late_quarters[0], late_bf[0])
        quantise_result(first, first_bf)
        quantise_result(late_quarters[1], late_bf[1])
        nc.scalar.dma_start(words_out[:, : S - QUARTER], o_w[:, : S - QUARTER].bitcast(I32))
        nc.sync.dma_start(words_out[:, S - QUARTER :], o_w[:, S - QUARTER :].bitcast(I32))
        for r in range(PACK):
            queue = nc.sync if r % 2 == 0 else nc.scalar
            queue.dma_start(out_2[0, r:SCALE_ROWS:PACK, :].bitcast(I32), o_s[r:P:QUADRANT, :].bitcast(I32))
